import numpy as np, ml_dtypes
CORES = [10,34,74,98]
N = 4
import mx_ref
BF = ml_dtypes.bfloat16
def gentries(a):
    return np.ascontiguousarray(a.reshape(8, 16, -1).transpose(0, 2, 1)).reshape(8, -1)
def gtable(e):
    e = np.asarray(e); return np.ascontiguousarray(e.reshape(8, -1, 16).transpose(0, 2, 1)).reshape(128, -1).astype(np.int32)
def gcols(t, e):
    v = np.concatenate([t.reshape(8, 16, -1, 4), np.zeros((8, 16, 1, 4), BF)], axis=2)
    return np.ascontiguousarray(np.stack([v[g][:, e[g]] for g in range(8)])).reshape(128, -1)
def tile(rs):
    return np.stack(rs, axis=2).reshape(128, -1).astype(BF)
def pick(q, e):
    c = np.concatenate([q[0].reshape(128, -1, 4), np.zeros((128, 1, 4), np.uint8)], axis=1); s = np.concatenate([q[1], np.ones((16, 1), np.uint8)], axis=1)
    return (np.ascontiguousarray(c[:, e].reshape(128, -1)), np.ascontiguousarray(s[:, e]))
def join(*qs):
    return (np.concatenate([q[0] for q in qs], axis=1), np.concatenate([q[1] for q in qs], axis=1))
def put(q, e, v):
    c, s = q[0].reshape(128, -1, 4).copy(), q[1].copy(); c[:, e] = v[0].reshape(128, -1, 4); s[:, e] = v[1]
    return (c.reshape(128, -1), s)
def pk(c, s):
    return (np.ascontiguousarray(c), mx_ref.live(s))
def emit(q):
    return q[0], q[1]
def packed(v, rng):
    q = [mx_ref.quantize(np.ascontiguousarray(v[r])) for r in range(N)]
    return np.stack([a for a, b in q]), np.stack([mx_ref.plane(b, rng) for a, b in q])
def values_of_codes():
    e, c = np.zeros((128, 128, 4), np.float32), np.zeros((128, 2, 4), np.uint8)
    e[np.arange(128), np.arange(128), 0] = 1
    c[:127, :, 0] = np.arange(256).reshape(2, 128).T[:127]
    return mx_ref.matmul(mx_ref.quantize(e.reshape(128, 512).astype(BF)), (c.reshape(128, 8), np.full((16, 2), 127, np.uint8))).T.reshape(-1).astype(np.float64)
CODE_VALUE, SCALE_VALUE = values_of_codes(), 2.0 ** (np.arange(256) - 127.0)
def decode(q):
    return (CODE_VALUE[q[0]].reshape(16, 8, -1, 4) * SCALE_VALUE[q[1]][:, None, :, None] + 0.0).reshape(128, -1).astype(np.float32)
def f(rng, *shape):
    return mx_ref.flush((rng.standard_normal(shape, dtype=np.float32) * np.exp2(rng.integers(-2, 3, shape[:-1] + (1,)))).astype(BF))
def wide(rng, *shape, cols=0):
    v = rng.standard_normal(shape, dtype=np.float32) * np.exp2(rng.integers(-12, 13, shape)).astype(np.float32)
    if cols: v *= np.repeat(np.exp2(rng.integers(-cols, cols + 1, shape[:-2] + (1, shape[-1] // 4))) * (rng.random(shape[:-2] + (1, shape[-1] // 4)) > 0.0625), 4, axis=-1).astype(np.float32)
    return mx_ref.flush(v.astype(BF))
C = 320
STEP = [1, 2, 3]
HOPS = 128
def numbers_of(rng):
    return {"x": np.array(f(rng, N, 128, 4 * C)), "u": np.array(f(rng, N, 128, 512)), "v": np.array(f(rng, N, 128, 512))}
def orders(rng):
    e = np.tile(np.arange(C), (N, 8, 1))
    k, a, t = rng.permuted(e, axis=2), rng.permuted(e, axis=2)[:, :, 16:], e.copy()
    np.put_along_axis(t, a[:, :, 0::2], a[:, :, 1::2], axis=2)
    np.put_along_axis(t, a[:, :, 1::2], a[:, :, 0::2], axis=2)
    return k, t
def stored(k, t):
    return {"nx": np.stack([gtable(k[r]) for r in range(N)]), "mt": np.stack([gtable(t[r]) for r in range(N)])}
def layers(rng, still=[]):
    w = np.array(f(rng, N, 128, 2048)).reshape(N, 8, 16, 4, 8, 16, 4)
    for i in still:
        w[:, :, i] = 0
        w[:, :, :, :, :, i] = 0
    return w
def weights(rng, w):
    c, p = packed(np.ascontiguousarray(w).reshape(N, 128, 2048), rng)
    return {"wc": c, "ws": p}
def setup_inputs(rng):
    return {**numbers_of(rng), **stored(*orders(rng)), **weights(rng, layers(rng))}
def setup_inputs_ties(rng):
    d = numbers_of(rng)
    k, t = orders(rng)
    o = rng.permutation(N) % 4
    n = rng.integers(0, 4, (N, 8, C))
    c = np.ones((N, 8), np.float32)
    for r in range(N):
        c[r] = rng.permutation(8) % 2 * 2.0 - 1.0
        for g in range(8):
            if o[r] < 2:
                e = rng.permutation(C)
                a = np.arange(C) + 1 if c[r, g] < 0 else C - np.arange(C)
                n[r, g, e] = a if o[r] == 0 else (a + 1) // 2
                k[r, g, e] = np.roll(e, -1)
            if o[r] == 3: n[r, g] = rng.integers(0, 2, C) if g % 2 else 1
        if o[r] < 2: t[r, rng.permutation(8)[:4]] = np.arange(C)
    digits = (n[..., None] & (1 << np.arange(12))).reshape(N, 8, C, 3, 4)
    x = d["x"].reshape(N, 8, 16, C, 4)
    x[:, :, 8:] = 0
    x[:, :, 8:11] = digits.transpose(0, 1, 3, 2, 4).astype(np.float32).astype(BF)
    u = d["u"].reshape(N, 128, 128, 4)
    u[:, :, ::16] = 0
    for g in range(8): u[:, 16 * g + 8:16 * g + 11, 16 * g] = c[:, g].astype(BF)[:, None, None]
    w = layers(rng)
    w[:, :, :, :, :, 8:] = 0
    return {"x": x.reshape(N, 128, 4 * C), "u": u.reshape(N, 128, 512), "v": d["v"], **stored(k, t), **weights(rng, w)}
def setup_inputs_near(rng):
    d = numbers_of(rng)
    x = d["x"].astype(np.float32).reshape(N, 8, 16, C, 4)
    x[:, :, :2] = 0
    x[:, :, 8:] = 0
    u = d["u"].reshape(N, 128, 128, 4)
    u[:, :, ::16] = 0
    w = layers(rng, [0, 1, 8, 9, 10, 11, 12, 13, 14, 15])
    o = (np.arange(N) + rng.integers(N)) % 4
    for r in range(N):
        c = rng.choice([-1.0, 1.0], (8, 1))
        s = rng.integers(0, 16, (8, C))
        digits = ((s[:, :, None] >> np.arange(4)) & 1) * np.exp2(np.arange(4) - 23.0)
        if o[r] < 2:
            x[r, :, 0, :, 0] = c
            x[r, :, 8] = digits
            x[r, :, 11, :, 0] = 2.0 ** -10
        else:
            x[r, :, :8] = 0
            x[r, :, 13, :, 0] = 2.0 ** -30
            x[r, :, 1, :, 0] = rng.choice([-1.0, 1.0], (8, C)) * 2.0 ** -30
            w[r] = 0
            for g in range(8): w[r, g, 1, 0, g, 12, 0] = 2.0 ** -8
        if o[r] == 2: x[r, :, 8] = digits * rng.choice([-1.0, 1.0], (8, C, 1))
        if o[r] == 3:
            x[r, :, 8, :, 0] = np.where(s < 8, 1.25, 0.0) * 2.0 ** -30 * c
            x[r, :, 9, :, 0] = np.where(s < 8, 0.0, 1.125) * 2.0 ** -30 * c
            for g in rng.permutation(8)[:4]:
                e = rng.choice([-1.0, 1.0], C) * 2.0 ** -30
                x[r, g, 8, :, 0] = 1.25 * e
                x[r, g, 9, :, 0] = -1.125 * e
        at = [0, C - 1, int(rng.integers(C)), int(rng.integers(C))]
        for g, j in zip(rng.permutation(8)[:4], at): x[r, g, 0, j, 0] = 2.0 ** 29 * rng.choice([-1.0, 1.0])
        k = 1.0 if o[r] == 0 else 2.0 ** -30
        for h in range(0, 128, 16):
            u[r, h, h, 0] = k if o[r] < 2 else 1.0
            if o[r] < 2: u[r, h + 11, h, 0] = k
            if o[r] < 3: u[r, h + 8, h] = k
            else:
                u[r, h + 8, h, 0] = k
                u[r, h + 9, h, 0] = 1.125 * k
                u[r, h + 12, h, 0] = k
    return {"x": x.reshape(N, 128, 4 * C).astype(BF), "u": u.reshape(N, 128, 512), "v": d["v"], **stored(*orders(rng)), **weights(rng, w)}
def setup_inputs_odd(rng):
    d = numbers_of(rng)
    w = layers(rng, [0, 8])
    x = (1.0 + (2 * rng.integers(0, 64, (N, 16, 8, C, 4)) + 1) * 2.0 ** -7) * np.exp2(-rng.integers(0, 7, (N, 16, 8, C, 4)).astype(np.float64)) * rng.choice([-1.0, 1.0], (N, 16, 8, C, 4))
    x[:, 0::2, 0, :, 0] = 1.96875 * 2.0 ** 8 * rng.choice([-1.0, 1.0], (8, 1))
    x[:, 1::2, 0, :, 0] = rng.choice([1.96875 * 2.0 ** 8, 8.0], (N, 8, C)) * rng.choice([-1.0, 1.0], (N, 8, C))
    for g in range(8): w[:, g, 0, 0, g, 0, 0] = -0.5
    u = d["u"].reshape(N, 16, 8, 128, 4)
    u[:, :, 0, ::16] = 0
    for r in rng.permutation(N)[:N // 2]:
        for i, g in enumerate(rng.permutation(8)[:4]):
            x[r, 2 * g, 1, :, 0] = (8 + rng.integers(0, 2, C)) * 2.0 ** (i - 8)
            u[r, :, :, 16 * g] = 0
            u[r, 2 * g, 1, 16 * g, 0] = 1.0
            w[r, :, :, 0, g, 1] = 0
    return {"x": x.astype(np.float32).reshape(N, 128, 4 * C).astype(BF), "u": u.reshape(N, 128, 512), "v": d["v"], **stored(*orders(rng)), **weights(rng, w)}
def setup_inputs_ends(rng):
    d = numbers_of(rng)
    k, t = orders(rng)
    o, e, m = rng.permutation(N) % 4, rng.permutation(N) % 4, rng.permutation(N) % 4
    for r in range(N):
        s = (r - STEP[-1]) % N
        if o[r] == 3 and o[s] == 2:
            a = rng.choice([n for n in range(N) if o[n] < 2 and o[(n + STEP[-1]) % N] != 3])
            o[s] = o[a]
            o[a] = 2
    i = np.arange(C)
    k[e == 0] = i
    k[e == 1] = (i + 1) % C
    k[e == 2] = C - 1 - i
    k[e == 3] = (i - 1) % C
    t[m == 0] = i
    t[m == 1] = C - 1 - i
    t[m == 2] = i ^ 1
    x = np.zeros((N, 8, 16, C, 4))
    u = d["u"].astype(np.float32).reshape(N, 128, 128, 4)
    v = d["v"].astype(np.float32)
    w = np.zeros((N, 128, 4, 128, 4), np.float32)
    j = np.arange(128)
    for r in range(N):
        h = rng.permutation(8)
        c = np.where(h < 2, 0.0, h % 2 * 2.0 - 1.0)[None, :, None]
        low = -(0.7 + 0.1 * rng.random((8, 16, C, 4))) * 2.0 ** 30
        if o[r] == 0: x[r] = low
        if o[r] == 1: x[r] = low * rng.choice([-1.0, 1.0], (C, 1))
        if o[r] == 2: x[r] = -(1.0 + 0.125 * rng.integers(0, 8, (8, 16, C, 4))) * 2.0 ** -30
        if o[r] == 3: x[r] = d["x"][r].astype(np.float32).reshape(8, 16, C, 4)[:, :, :1]
        if o[r] < 2:
            u[r, :, ::16] = c * (0.9 + 0.1 * rng.random((128, 8, 4))) * 2.0 ** 30
            v[r] = rng.choice([-1.0, 1.0], (128, 512)) * (0.9 + 0.1 * rng.random((128, 512))) * 2.0 ** 30
        if o[r] == 2:
            u[r, :, ::16] = c * (1.0 + 0.125 * rng.integers(0, 8, (128, 8, 4))) * 2.0 ** -30
            v[r] = rng.choice([-1.0, 1.0], (128, 512)) * (1.0 + 0.125 * rng.integers(0, 8, (128, 512))) * 2.0 ** -30
        if o[r] == 3: u[r, :, ::16] *= np.abs(c).astype(np.float32)
        a = np.array([2.0, 2.0 ** -8, -0.25])[rng.permutation(8) % 3][j // 16]
        if o[r] == 2: a = np.zeros(128)
        a[120:] = 256.0
        for b in range(4): w[r, j, b, j, b] = a
    x[:, 7, 8:] = -2.0 ** -30
    return {"x": x.astype(np.float32).reshape(N, 128, 4 * C).astype(BF), "u": u.reshape(N, 128, 512).astype(BF), "v": v.astype(BF), **stored(k, t), **weights(rng, w.astype(BF))}
def setup_inputs_spread(rng):
    d = setup_inputs(rng)
    d["x"] = wide(rng, N, 128, 4 * C, cols=6)
    return d
def check_inputs(d):
    b = []
    for k in ("x", "u", "v"):
        a = np.abs(d[k].astype(np.float32))
        if not (np.isfinite(a).all() and ((a == 0) | (a >= 2.0 ** -30) & (a <= 2.0 ** 30)).all()): b.append("a value of " + k)
    none, least, most = [emit(mx_ref.quantize(np.full((128, 16), k, np.float32).astype(BF)))[1][0, 0] for k in (0.0, 2.0 ** -8, 2.0 ** 8)]
    for r in range(N):
        k, t = gentries(d["nx"][r]), gentries(d["mt"][r])
        if not (np.sort(k, axis=1) == np.arange(C)).all(): b.append("nx: not every column once")
        if not (((t >= 0) & (t < C)).all() and (np.take_along_axis(t, np.clip(t, 0, C - 1), axis=1) == np.arange(C)).all()): b.append("mt: not each other's")
        if ((d["wc"][r] == 0x7F) | (d["wc"][r] == 0xFF)).any(): b.append("wc: a code that is no number")
        s = mx_ref.live(d["ws"][r])
        if ((s != none) & ((s < least) | (s > most))).any(): b.append("ws: a scale out of range")
        if (((d["wc"][r].reshape(16, 8, 512, 4) & 0x7F) != 0) & (s == none)[:, None, :, None]).any(): b.append("wc: a code other than zero under the scale of zeros")
    return b
def at(a, e):
    return np.take_along_axis(a, e, axis=1)
def search(s, follow):
    b = np.tile(np.arange(C), (8, 1))
    p, left = b.copy(), np.ones((8, C), bool)
    for hop in range(1, HOPS + 1):
        to = at(follow, p)
        larger = left & (at(s, to) > s)
        b = np.where(larger, to, b)
        left = left & ~larger
        if hop < HOPS: p = np.where(left, to, p)
    return b, p
def layer(w, q):
    return tile([mx_ref.matmul(pick(w, np.arange(128 * k, 128 * k + 128)), q) * np.float32(0.03125) for k in range(4)])
def reference(x, u, v, nx, mt, wc, ws):
    qu = [mx_ref.quantize(u[r]) for r in range(N)]
    lay = [pk(wc[r], ws[r]) for r in range(N)]
    follow, mate = [gentries(nx[r]) for r in range(N)], [gentries(mt[r]) for r in range(N)]
    now = [x[r] for r in range(N)]
    for step in STEP:
        t, z, first = [], [], []
        for r in range(N):
            q = mx_ref.quantize(now[r])
            s = mx_ref.matmul(qu[r], q)[::16] + np.float32(0.0)
            b, p = search(s, follow[r])
            t.append(decode(q))
            c = t[r].astype(BF)
            z.append(mx_ref.quantize(((gcols(c, b).astype(np.float32) + gcols(c, p).astype(np.float32)) * np.float32(0.5)).astype(BF)))
            first.append(b)
            e = at(s, b)
            swap = at(e, np.minimum(mate[r], np.arange(C))) > at(e, np.maximum(mate[r], np.arange(C)))
            follow[r] = np.where(swap, at(follow[r], mate[r]), follow[r])
        now = [(t[r] + gcols(layer(lay[r], z[(r - step) % N]), first[r]).astype(np.float32)).astype(BF) for r in range(N)]
    y, nf = np.zeros((N, 128, C), np.float32), np.zeros((N, 8, C), np.float32)
    oc, osc = np.zeros((N, 128, 4 * C), np.uint8), np.zeros((N, 16, C), np.uint8)
    for r in range(N):
        q = mx_ref.quantize(now[r])
        y[r] = mx_ref.matmul(mx_ref.quantize(v[r]), q)
        nf[r] = follow[r]
        oc[r], osc[r] = emit(q)
    return {"y": y, "nf": nf, "oc": oc, "osc": osc}

@@ -1,0 +1,448 @@
+from concourse.mybir import dt, AluOpType, ActivationFunctionType
+A = AluOpType
+AF = ActivationFunctionType
+C = 320
+BANK = 512
+ROUNDS = 3
+BIG = 1e29
+GROUPS = [[6, 5], [4, 3], [2, 1], [0, -1]]
+
+SCRATCH = {
+    "x0": ("sbuf", [128, 4 * C], "bfloat16"), "ut": ("sbuf", [128, 512], "bfloat16"), "vt": ("sbuf", [128, 512], "bfloat16"),
+    "nxi": ("sbuf", [128, 20], "int32"), "mti": ("sbuf", [128, 20], "int32"),
+    "wq": ("sbuf", [128, 512], "float8_e4m3fn_x4"), "wp": ("sbuf", [128, 512], "uint8"),
+    "uq": ("sbuf", [128, 128], "float8_e4m3fn_x4"), "up": ("sbuf", [128, 128], "uint8"),
+    "uqr": ("sbuf", [128, 128], "float8_e4m3fn_x4"), "upr": ("sbuf", [128, 128], "uint8"),
+    "vq": ("sbuf", [128, 128], "float8_e4m3fn_x4"), "vp": ("sbuf", [128, 128], "uint8"),
+    "eq": ("sbuf", [128, 512], "float8_e4m3fn_x4"), "ep": ("sbuf", [128, 512], "uint8"),
+    "one": ("sbuf", [128, 528], "bfloat16"), "big": ("sbuf", [128, 528], "bfloat16"),
+    "ji": ("sbuf", [128, C], "int32"), "dg": ("sbuf", [128, C], "int32"), "t1": ("sbuf", [128, C], "float32"), "t2": ("sbuf", [128, C], "float32"),
+    "rs0": ("sbuf", [128, C], "bfloat16"), "rs": ("sbuf", [128, C], "bfloat16"), "wt": ("sbuf", [128, C], "bfloat16"),
+    "mask": ("sbuf", [128, C], "bfloat16"), "cap": ("sbuf", [128, C], "float32"), "idr": ("sbuf", [128, C], "bfloat16"),
+    "pi": ("sbuf", [128, 20], "int32"), "pa15": ("sbuf", [128, 20], "int32"), "ci": ("sbuf", [128, 20], "int32"),
+    "ui": ("sbuf", [128, 8], "int32"), "uo": ("sbuf", [128, 8], "uint16"),
+    "mt16": ("sbuf", [128, 20], "uint16"), "lo16": ("sbuf", [128, 20], "uint16"), "hi16": ("sbuf", [128, 20], "uint16"),
+    "srow": ("sbuf", [128, C], "float32"), "sm": ("sbuf", [128, C], "float32"),
+    "d0": ("sbuf", [128, C], "float32"), "d1": ("sbuf", [128, C], "float32"),
+    "cb": ("sbuf", [128, C], "bfloat16"), "cs": ("sbuf", [128, C], "bfloat16"),
+    "pb": ("sbuf", [128, C], "bfloat16"), "psn": ("sbuf", [128, C], "bfloat16"),
+    "fb": ("sbuf", [128, C], "bfloat16"), "fsn": ("sbuf", [128, C], "bfloat16"),
+    "o0": ("sbuf", [128, 20], "uint16"), "o1": ("sbuf", [128, 20], "uint16"), "o3": ("sbuf", [128, 20], "uint16"),
+    "er": ("sbuf", [128, C], "float32"), "eh": ("sbuf", [128, C], "float32"), "sw": ("sbuf", [128, C], "bfloat16"),
+    "scn": ("sbuf", [128, C], "float32"), "swn": ("sbuf", [128, C], "float32"), "fmn": ("sbuf", [128, C], "float32"), "fmr": ("sbuf", [128, C], "bfloat16"),
+    "fo": ("sbuf", [128, 4 * C], "bfloat16"), "fh": ("sbuf", [128, 4 * C], "bfloat16"), "gp": ("sbuf", [128, 4 * C], "bfloat16"),
+    "z": ("sbuf", [128, 4 * C], "bfloat16"), "zq": ("sbuf", [128, C], "float8_e4m3fn_x4"), "zp": ("sbuf", [128, C], "uint8"),
+    "h": ("sbuf", [128, 4 * C], "bfloat16"),
+    "pu": ("psum", [128, 2048], "float32"), "pw": ("psum", [128, 2048], "float32"),
+}
+LISTS = ["cw", "cwc", "cwu", "col", "f0", "f1", "h0", "h1", "pif", "bd", "be", "bf", "swc", "fmv", "fw", "fd", "fe", "fn"]
+SCRATCH["sml"] = ("sbuf", [128, 20 * len(LISTS)], "float32")
+TABLES = {}
+for _i, _l in enumerate(GROUPS):
+    SCRATCH["p%d" % _i] = ("sbuf", [128, C * 2 ** len(_l)], "bfloat16")
+    for _j, _k in enumerate(_l):
+        TABLES[_k] = "m%d" % _k if _k >= 0 else "ml"
+        SCRATCH[TABLES[_k]] = ("sbuf", [128, C * 2 ** _j], "float32")
+SCRATCH["pn"] = ("sbuf", [128, C * 2 ** (len(GROUPS[-1]) - 1)], "bfloat16")
+for _k in range(7):
+    SCRATCH["l%d" % _k] = ("sbuf", [128, 20], "uint16")
+    SCRATCH["F%d" % _k] = ("sbuf", [128, C], "bfloat16")
+for _r in range(ROUNDS + 1):
+    if _r:
+        SCRATCH["x%d" % _r] = ("sbuf", [128, 4 * C], "bfloat16")
+    SCRATCH["xq%d" % _r] = ("sbuf", [128, C], "float8_e4m3fn_x4")
+    SCRATCH["xp%d" % _r] = ("sbuf", [128, C], "uint8")
+for _r in range(ROUNDS):
+    SCRATCH["aq%d" % _r] = ("sbuf", [128, C], "float8_e4m3fn_x4")
+    SCRATCH["ap%d" % _r] = ("sbuf", [128, C], "uint8")
+    for _n in ("lp", "lb", "rp", "rb"):
+        SCRATCH["%s%d" % (_n, _r)] = ("sbuf", [128, 20], "uint16")
+SEMAPHORES = ["ev", "es", "et", "eg", "snd", "st"]
+SEMAPHORES += ["%s%d" % (_n, _r) for _n in ("ax", "arp", "arb") for _r in range(ROUNDS)]
+SEMAPHORES += ["ld_" + _n for _n in ("x", "u", "v", "nx", "mt", "wc", "ws")]
+
+GATHER, SCAN2, SCAN4, ROW, SMALL = 0.58, 0.17, 0.33, 0.34, 0.08
+HOP, SAME = 0.12, 0.06
+
+
+def new_plan():
+    return {"tasks": [], "w": {}, "r": {}}
+
+
+def overlap(a, b):
+    return a[0] < b[1] and b[0] < a[1]
+
+
+def task(P, eng, dur, fn, reads, writes, kind="op", sem=None, inc=1, after=()):
+    def reg(x):
+        return (x, 0, 1 << 20) if isinstance(x, str) else x
+    n = len(P["tasks"])
+    deps = {}
+    for a in after:
+        deps[a] = True
+    rd, wr = [reg(x) for x in reads], [reg(x) for x in writes]
+    for b, lo, hi in rd:
+        for (l, h, t) in P["w"].get(b, []):
+            if overlap((lo, hi), (l, h)):
+                deps[t] = True
+        if b in ("pu", "pw"):
+            for (l, h, t) in P["r"].get(b, []):
+                if overlap((lo, hi), (l, h)) and P["tasks"][t]["eng"] != eng:
+                    deps.setdefault(t, False)
+    for b, lo, hi in wr:
+        for (l, h, t) in P["w"].get(b, []):
+            if overlap((lo, hi), (l, h)):
+                deps[t] = True
+        for (l, h, t) in P["r"].get(b, []):
+            if overlap((lo, hi), (l, h)):
+                deps.setdefault(t, False)
+    for b, lo, hi in wr:
+        P["w"][b] = [e for e in P["w"].get(b, []) if not (lo <= e[0] and e[1] <= hi)] + [(lo, hi, n)]
+        P["r"][b] = [e for e in P["r"].get(b, []) if not (lo <= e[0] and e[1] <= hi)]
+    for b, lo, hi in rd:
+        P["r"].setdefault(b, []).append((lo, hi, n))
+    deps.pop(n, None)
+    P["tasks"].append({"eng": eng, "dur": dur, "fn": fn, "deps": deps, "kind": kind, "sem": sem, "inc": inc})
+    return n
+
+
+def schedule(P):
+    ts = P["tasks"]
+    n = len(ts)
+    succ = [[] for _ in range(n)]
+    for i, t in enumerate(ts):
+        for d in t["deps"]:
+            succ[d].append(i)
+
+    def lag(d, i):
+        return SAME if ts[d]["eng"] == ts[i]["eng"] else HOP
+    up = [0.0] * n
+    for i in range(n - 1, -1, -1):
+        up[i] = ts[i]["dur"] + max([up[s] + lag(i, s) for s in succ[i]] or [0.0])
+    left = [len(t["deps"]) for t in ts]
+    ready = [i for i in range(n) if left[i] == 0]
+    slots = {}
+    start, end = [0.0] * n, [0.0] * n
+    while ready:
+        i = max(ready, key=lambda k: (up[k], -k))
+        ready.remove(i)
+        t = ts[i]
+        at = max([end[d] + lag(d, i) for d in t["deps"]] or [0.0])
+        if t["eng"] != "net":
+            line = slots.setdefault(t["eng"], [])
+            k = 0
+            for k in range(len(line) + 1):
+                s = max(at, line[k - 1][1] if k else 0.0)
+                if k == len(line) or s + t["dur"] <= line[k][0] + 1e-9:
+                    break
+            line.insert(k, (s, s + t["dur"], i))
+            at = s
+        start[i], end[i] = at, at + t["dur"]
+        for s in succ[i]:
+            left[s] -= 1
+            if left[s] == 0:
+                ready.append(s)
+    return {e: [x[2] for x in line] for e, line in slots.items()}, start, end
+
+
+def issue(P, order, start, g, T):
+    ts = P["tasks"]
+    queue = {"v": g.vector, "s": g.scalar, "t": g.tensor, "g": g, "y": g.sync}
+    counter = {"v": "ev", "s": "es", "t": "et", "g": "eg"}
+    mark, count = {}, {}
+    for e, line in order.items():
+        for i in line:
+            t = ts[i]
+            if t["kind"] == "op":
+                count[counter[e]] = count.get(counter[e], 0) + 1
+                mark[i] = (counter[e], count[counter[e]])
+            else:
+                mark[i] = (t["sem"], t["inc"])
+    for i, t in enumerate(ts):
+        if t["kind"] == "land":
+            mark[i] = (t["sem"], t["inc"])
+    seen = {e: {} for e in queue}
+    known = {}
+    pos = {i: k for line in order.values() for k, i in enumerate(line)}
+    for i in sorted(pos, key=lambda i: (start[i], pos[i])):
+        t = ts[i]
+        e = t["eng"]
+        q, have = queue[e], seen[e]
+        need = {}
+        for d, result in t["deps"].items():
+            if ts[d]["kind"] == "send" or (ts[d]["eng"] == e and not result and ts[d]["kind"] == "op"):
+                continue
+            s, v = mark[d]
+            need[s] = max(need.get(s, 0), v)
+        for s, v in sorted(need.items()):
+            if have.get(s, 0) < v:
+                q.wait_ge(T.sem[s], v)
+                have[s] = v
+        for d, result in t["deps"].items():
+            if d in known and not (ts[d]["eng"] == e and not result):
+                for s, v in known[d].items():
+                    have[s] = max(have.get(s, 0), v)
+        k = dict(have)
+        if t["kind"] == "op":
+            t["fn"](q).then_inc(T.sem[mark[i][0]], 1)
+            k[mark[i][0]] = max(k.get(mark[i][0], 0), mark[i][1])
+        elif t["kind"] == "dma":
+            t["fn"](q).then_inc(T.sem[t["sem"]], 16)
+        else:
+            t["fn"](q)
+        if t["kind"] == "op":
+            known[i] = k
+    return count
+
+
+def build(P, g, core, T, topo):
+    rank = T.rank_of(core)
+    n = len(T.cores)
+    lists = {name: T.sml[:, 20 * i:20 * i + 20] for i, name in enumerate(LISTS)}
+    col = T.sml[:, 20 * LISTS.index("col"):20 * LISTS.index("col") + 1]
+
+    def L(name):
+        return lists[name]
+
+    def V(dur, fn, reads, writes):
+        return task(P, "v", dur, fn, reads, writes)
+
+    def S(dur, fn, reads, writes):
+        return task(P, "s", dur, fn, reads, writes)
+
+    def E(dur, fn, reads, writes):
+        return task(P, "t", dur, fn, reads, writes)
+
+    def K(dur, fn, reads, writes):
+        return task(P, "g", dur, fn, reads, writes)
+
+    def every16(b):
+        return T[b][:, 15:C:16]
+
+    def at(b, a):
+        return T[b][:, C * a:C * a + C]
+
+    def copy(q, out, in_, **kw):
+        return q.activation(out, in_, AF.Copy, **kw)
+
+    def load(q, name, fn, writes):
+        k = task(P, q, 0.07, fn, [], [], "dma", "ld_" + name, 16)
+        task(P, "net", 2.0, None, [], writes, "land", "ld_" + name, 16, after=[k])
+
+    load("y", "x", lambda q: q.dma_start(T.x0[:], T.x[:]), ["x0"])
+    load("s", "nx", lambda q: q.dma_start(T.nxi[:], T.nx[:]), ["nxi"])
+    load("y", "u", lambda q: q.dma_start(T.ut[:], T.u[:]), ["ut"])
+    load("s", "mt", lambda q: q.dma_start(T.mti[:], T.mt[:]), ["mti"])
+    load("y", "wc", lambda q: q.dma_start(T.wq[:].bitcast(dt.uint8), T.wc[:]), ["wq"])
+    load("y", "ws", lambda q: q.dma_start(T.wp[:], T.ws[:]), ["wp"])
+    load("y", "v", lambda q: q.dma_start(T.vt[:], T.v[:]), ["vt"])
+
+    K(0.67, lambda q: q.iota(T.ji[:], [[1, C]], 0, -1), [], ["ji"])
+    K(0.67, lambda q: q.iota(T.idr[:], [[1, C]], -160, 0, allow_small_or_imprecise_dtypes=True), [], ["idr"])
+    K(0.17, lambda q: q.iota(T.pi[:], [[0, 20]], 0, 1), [], ["pi"])
+    K(0.17, lambda q: q.iota(T.ci[:], [[16, 20]], 0, 0), [], ["ci"])
+    K(0.15, lambda q: q.iota(T.ui[:], [[16, 8]], 0, 0), [], ["ui"])
+    K(0.67, lambda q: q.iota(T.rs0[:], [[0, 20], [1, 16]], 0, 0, allow_small_or_imprecise_dtypes=True), [], ["rs0"])
+    V(0.3, lambda q: q.memset(T.one[:], 1.0), [], ["one"])
+    K(1.1, lambda q: q.affine_select(T.big[:], T.one[:], [[-1, 528]], A.is_equal, 0.0, 3, 4), ["one"], ["big"])
+    V(ROW, lambda q: q.tensor_scalar(T.dg[:], T.ji[:], 15, None, A.bitwise_and), ["ji"], ["dg"])
+    V(ROW, lambda q: q.tensor_scalar(T.t1[:], T.dg[:], 1.0, 65535.0, A.is_equal, A.mult), ["dg"], ["t1"])
+    V(ROW, lambda q: q.tensor_scalar(T.t2[:], T.dg[:], 0.0, None, A.not_equal), ["dg"], ["t2"])
+    V(2 * ROW, lambda q: q.tensor_tensor(T.wt[:], T.t1[:], T.t2[:], A.add), ["t1", "t2"], ["wt"])
+    V(ROW, lambda q: q.tensor_scalar(T.mask[:], T.dg[:], 0.0, None, A.is_equal), ["dg"], ["mask"])
+    V(ROW, lambda q: q.tensor_scalar(T.cap[:], T.mask[:], 2 * BIG, -BIG, A.mult, A.add), ["mask"], ["cap"])
+    V(ROW, lambda q: q.tensor_scalar(T.rs[:], T.rs0[:], 1.0, None, A.min), ["rs0"], ["rs"])
+    V(SMALL, lambda q: q.tensor_scalar(T.pa15[:], T.pi[:], 15, None, A.bitwise_and), ["pi"], ["pa15"])
+    V(SMALL, lambda q: q.tensor_scalar(L("f0"), T.pa15[:], 15.0, 1.0 - 2.0 ** -16, A.is_equal, A.mult), ["pa15"], ["f0"])
+    V(SMALL, lambda q: q.tensor_scalar(L("col"), L("f0"), 2.0 ** -16, None, A.add), ["f0"], ["col"])
+    V(SMALL, lambda q: q.tensor_tensor(L("cw"), T.pa15[:], T.ci[:], A.add), ["pa15", "ci"], ["cw"])
+    V(SMALL, lambda q: q.tensor_scalar(L("cwc"), L("cw"), -160.0, None, A.add), ["cw"], ["cwc"])
+    V(SMALL, lambda q: q.tensor_scalar(L("cwu"), L("cw"), 1.0 / C, None, A.mult), ["cw"], ["cwu"])
+    V(SMALL, lambda q: q.tensor_copy(T.uo[:], T.ui[:]), ["ui"], ["uo"])
+    for i in range(len(GROUPS)):
+        S(ROW, lambda q, i=i: copy(q, at("p%d" % i, 0), T.idr[:]), ["idr"], [("p%d" % i, 0, 1)])
+    for b in range(4):
+        V(0.16, lambda q, b=b: q.quantize_mx(T.eq[:, 128 * b:128 * b + 128], T.ep[:, 128 * b:128 * b + 128], T.big[:, 3 - b:515 - b]),
+          ["big"], [("eq", b, b + 1), ("ep", b, b + 1)])
+
+    V(0.16, lambda q: q.quantize_mx(T.uq[:], T.up[:], T.ut[:]), ["ut"], ["uq", "up"])
+    V(0.3, lambda q: q.tensor_copy(T.uqr[:].bitcast(dt.uint32), T.uq[:].bitcast(dt.uint32).indirect(T.uo[:])), ["uq", "uo"], ["uqr"])
+    V(0.3, lambda q: q.tensor_copy(T.upr[:], T.up[:].indirect(T.uo[:])), ["up", "uo"], ["upr"])
+    V(0.16, lambda q: q.quantize_mx(T.vq[:], T.vp[:], T.vt[:]), ["vt"], ["vq", "vp"])
+
+    V(SMALL, lambda q: q.tensor_copy(T.l0[:], T.nxi[:]), ["nxi"], ["l0"])
+    V(SMALL, lambda q: q.tensor_copy(T.mt16[:], T.mti[:]), ["mti"], ["mt16"])
+    V(SMALL, lambda q: q.tensor_copy(L("bd"), T.mti[:]), ["mti"], ["bd"])
+    V(SMALL, lambda q: q.tensor_tensor(L("be"), L("bd"), L("cw"), A.min), ["bd", "cw"], ["be"])
+    V(SMALL, lambda q: q.tensor_tensor(L("bf"), L("bd"), L("cw"), A.max), ["bd", "cw"], ["bf"])
+    V(SMALL, lambda q: q.tensor_copy(T.lo16[:], L("be")), ["be"], ["lo16"])
+    V(SMALL, lambda q: q.tensor_copy(T.hi16[:], L("bf")), ["bf"], ["hi16"])
+
+    def row(out, a, win, i, k):
+        S(GATHER, lambda q: copy(q, at(out, a), at(win, i).indirect(T["l%d" % k][:])), [(win, i, i + 1), "l%d" % k], [(out, a, a + 1)])
+
+    def masked(dst, win, i, k, off):
+        V(GATHER, lambda q: q.tensor_tensor(T[dst][:], T[win][:, C * i:C * k].indirect(T[off][:]), T.mask[:], A.mult), [(win, i, k), off, "mask"], [dst])
+
+    def running(dst, src):
+        V(SCAN2, lambda q: q.tensor_tensor_scan(T[dst][:], T.rs[:], T[src][:], 0.0, A.mult, A.add), ["rs", src], [dst])
+
+    def weighted(dst, src):
+        V(SCAN4, lambda q: q.tensor_tensor_scan(T[dst][:], T.wt[:], T[src][:], 0.0, A.mult, A.add), ["wt", src], [dst])
+
+    def powers(first):
+        row("F0", 0, "idr", 0, 0)
+        for k in range(6):
+            b, l = "F%d" % (k + 1), "l%d" % (k + 1)
+            if first:
+                masked("pb", "F%d" % k, 0, 1, "l%d" % k)
+                running("psn", "pb")
+                V(SMALL, lambda q, l=l: q.tensor_scalar(T[l][:], every16("psn"), 160.0, None, A.add), ["psn"], [l])
+            row(b, 0, "F%d" % k, 0, k)
+            if not first:
+                weighted("scn", b)
+                V(SMALL, lambda q, l=l: q.tensor_scalar(T[l][:], every16("scn"), col, 160.25, A.mult, A.add), ["scn", "col"], [l])
+        for i, levels in enumerate(GROUPS):
+            for j, k in enumerate(levels):
+                if k >= 0:
+                    for a in range(2 ** j):
+                        row("p%d" % i, 2 ** j + a, "p%d" % i, a, k)
+        for a in range(2 ** (len(GROUPS[-1]) - 1)):
+            row("pn", a, "p%d" % (len(GROUPS) - 1), a, 0)
+
+    sent = [0]
+
+    def send(r, pairs, sem, land, latency):
+        dst, src = T.cores[(rank + r + 1) % n], T.cores[(rank - r - 1) % n]
+        rid, pid, _ = topo.addr(dst)
+        m = topo.mask(core, dst)
+        ids = []
+        for out, in_, name in pairs:
+            ids.append(task(P, "g", 0.1, lambda q, out=out, in_=in_: q.remote_dma(out, in_, T.sem[sem], T.sem.snd, pid, rid, m), [name], [], "send"))
+            sent[0] += len(topo.engines(core, dst))
+        return task(P, "net", latency, None, [], land, "land", sem, len(topo.engines(src, core)) * len(pairs), after=ids)
+
+    def compare(level, off):
+        win = TABLES[level]
+        V(GATHER, lambda q: q.tensor_tensor(T.cb[:], T[win][:].indirect(T[off][:]), T.sm[:], A.is_le), [win, off, "sm"], ["cb"])
+
+    def mm(out, b, wq, wp, a, xq, xp, unit):
+        E(0.35, lambda q: q.matmul_mx(T[out][:, BANK * b:BANK * b + C], T[wq][:, a:a + 128], T[wp][:, a:a + 128], T[xq][:], T[xp][:], True, True),
+          [(wq, unit, unit + 1), (wp, unit, unit + 1), xq, xp], [(out, b, b + 1)])
+
+    def bank(out, b):
+        return T[out][:, BANK * b:BANK * b + C]
+
+    powers(False)
+    for r in range(ROUNDS):
+        X, xq, xp, aq, ap = "x%d" % r, "xq%d" % r, "xp%d" % r, "aq%d" % r, "ap%d" % r
+        lp, lb, rp, rb = "lp%d" % r, "lb%d" % r, "rp%d" % r, "rb%d" % r
+        V(0.37, lambda q, xq=xq, xp=xp, X=X: q.quantize_mx(T[xq][:], T[xp][:], T[X][:]), [X], [xq, xp])
+        send(r, [(T[aq][:].bitcast(dt.uint8), T[xq][:].bitcast(dt.uint8), xq), (T[ap][:], T[xp][:], xp)], "ax%d" % r, [aq, ap], 6.0)
+        mm("pw", 0, "uqr", "upr", 0, xq, xp, 0)
+        mm("pw", 1, "uqr", "upr", 0, xq, xp, 0)
+        S(ROW, lambda q: copy(q, T.srow[:], bank("pw", 0)), [("pw", 0, 1)], ["srow"])
+        V(ROW, lambda q: q.tensor_tensor(T.sm[:], bank("pw", 1), T.cap[:], A.min), [("pw", 1, 2), "cap"], ["sm"])
+        V(GATHER, lambda q: q.tensor_copy(at("m0", 0), T.srow[:].indirect(T.l0[:])), ["srow", "l0"], [("m0", 0, 1)])
+        S(GATHER, lambda q: copy(q, at("ml", 0), T.srow[:].indirect(T.l0[:])), ["srow", "l0"], [("ml", 0, 1)])
+        for k in range(6):
+            twin = "d%d" % (k % 2) if k else "ml"
+            if k:
+                V(ROW, lambda q, k=k, twin=twin: q.tensor_copy(at(twin, 0), at("m%d" % k, 0)), [("m%d" % k, 0, 1)], [(twin, 0, 1)])
+            V(GATHER, lambda q, k=k, twin=twin: q.tensor_tensor(at("m%d" % (k + 1), 0), at("m%d" % k, 0).indirect(T["l%d" % k][:]), at(twin, 0), A.max),
+              [("m%d" % k, 0, 1), (twin, 0, 1), "l%d" % k], [("m%d" % (k + 1), 0, 1)])
+        for levels in GROUPS:
+            for i, k in enumerate(levels):
+                for j in range(i):
+                    for a in range(2 ** j):
+                        row(TABLES[k], 2 ** j + a, TABLES[k], a, levels[j])
+        for b in range(4):
+            mm("pu", b, "eq", "ep", 128 * b, xq, xp, b)
+            S(ROW, lambda q, b=b: copy(q, at("fo", b), bank("pu", b)), [("pu", b, b + 1)], [("fo", b, b + 1)])
+        for b in range(4):
+            mm("pu", b, "eq", "ep", 128 * b, aq, ap, b)
+            S(ROW, lambda q, b=b: copy(q, at("fh", b), bank("pu", b), scale=0.5), [("pu", b, b + 1)], [("fh", b, b + 1)])
+        for i, levels in enumerate(GROUPS):
+            place, off, last = "cwu" if i == 0 else "pif", "o3", i == len(GROUPS) - 1
+            for j, k in enumerate(levels):
+                if i == 0 and j == 0:
+                    V(2 * ROW, lambda q: q.tensor_tensor(T.cb[:], at("m6", 0), T.sm[:], A.is_le), [("m6", 0, 1), "sm"], ["cb"])
+                else:
+                    compare(k, off)
+                running("cs", "cb")
+                if k < 0:
+                    break
+                f, off = "f%d" % (j % 2), "o%d" % (j % 2)
+                V(SMALL, lambda q, f=f, place=place: q.tensor_tensor(L(f), L(place), every16("cs"), A.add), [place, "cs"], [f])
+                V(SMALL, lambda q, f=f, off=off, j=j: q.tensor_scalar(T[off][:], L(f), float(C * 2 ** j), 0.25, A.mult, A.add), [f], [off])
+                if j + 1 < len(levels) and levels[j + 1] >= 0:
+                    place = "h%d" % (j % 2)
+                    S(0.1, lambda q, f=f, place=place: copy(q, L(place), L(f), scale=0.5), [f], [place])
+                if j + 1 < len(levels) and levels[j + 1] < 0:
+                    masked("pb", "p%d" % i, 0, 2 ** (j + 1), off)
+                    running("psn", "pb")
+                    V(SMALL, lambda q, lp=lp: q.tensor_scalar(T[lp][:], every16("psn"), 160.0, None, A.add), ["psn"], [lp])
+                    send(r, [(T[rp][:], T[lp][:], lp)], "arp%d" % r, [rp], 2.6)
+                    masked("fb", "pn", 0, 2 ** (j + 1), off)
+                    running("fsn", "fb")
+                    V(SMALL, lambda q: q.tensor_tensor(L("bd"), L("cwc"), every16("fsn"), A.subtract), ["cwc", "fsn"], ["bd"])
+            if not last:
+                masked("pb", "p%d" % i, 0, 2 ** len(levels), off)
+                running("psn", "pb")
+                V(SMALL, lambda q: q.tensor_scalar(T.o3[:], every16("psn"), 160.0, None, A.add), ["psn"], ["o3"])
+                S(0.1, lambda q: copy(q, L("pif"), every16("psn"), scale=1.0 / C, bias=160.0 / C), ["psn"], ["pif"])
+        V(SMALL, lambda q: q.tensor_tensor(L("be"), L("bd"), every16("cs"), A.mult), ["bd", "cs"], ["be"])
+        V(SMALL, lambda q: q.tensor_tensor(L("bf"), L("be"), every16("fsn"), A.add), ["be", "fsn"], ["bf"])
+        V(SMALL, lambda q, lb=lb: q.tensor_scalar(T[lb][:], L("bf"), 160.0, None, A.add), ["bf"], [lb])
+        send(r, [(T[rb][:], T[lb][:], lb)], "arb%d" % r, [rb], 2.6)
+        S(GATHER, lambda q, lb=lb: copy(q, T.er[:], T.srow[:].indirect(T[lb][:])), ["srow", lb], ["er"])
+        S(GATHER, lambda q: copy(q, T.eh[:], T.er[:].indirect(T.hi16[:])), ["er", "hi16"], ["eh"])
+        V(GATHER, lambda q: q.tensor_tensor(T.sw[:], T.er[:].indirect(T.lo16[:]), T.eh[:], A.is_gt), ["er", "eh", "lo16"], ["sw"])
+        weighted("swn", "sw")
+        V(SMALL, lambda q: q.tensor_scalar(L("swc"), every16("swn"), col, 0.5, A.mult, A.is_ge), ["swn", "col"], ["swc"])
+        S(GATHER, lambda q: copy(q, T.fmr[:], T.F0[:].indirect(T.mt16[:])), ["F0", "mt16"], ["fmr"])
+        weighted("fmn", "fmr")
+        V(SMALL, lambda q: q.tensor_scalar(L("fmv"), every16("fmn"), col, 160.0, A.mult, A.add), ["fmn", "col"], ["fmv"])
+        V(SMALL, lambda q: q.tensor_copy(L("fw"), T.l0[:]), ["l0"], ["fw"])
+        V(SMALL, lambda q: q.tensor_tensor(L("fd"), L("fmv"), L("fw"), A.subtract), ["fmv", "fw"], ["fd"])
+        V(SMALL, lambda q: q.tensor_tensor(L("fe"), L("fd"), L("swc"), A.mult), ["fd", "swc"], ["fe"])
+        V(SMALL, lambda q: q.tensor_tensor(L("fn"), L("fw"), L("fe"), A.add), ["fw", "fe"], ["fn"])
+        V(SMALL, lambda q: q.tensor_scalar(T.l0[:], L("fn"), 0.25, None, A.add), ["fn"], ["l0"])
+        if r < ROUNDS - 1:
+            powers(False)
+        else:
+            S(GATHER, lambda q: copy(q, T.er[:], T.idr[:].indirect(T.l0[:]), bias=160.0), ["idr", "l0"], ["er"])
+            task(P, "y", 0.07, lambda q: q.dma_start(T.nf[:], T.er[0:128:16, :]), ["er"], [], "dma", "st", 16)
+        for b in range(4):
+            S(GATHER, lambda q, b=b, rp=rp: copy(q, at("gp", b), at("fh", b).indirect(T[rp][:])), [("fh", b, b + 1), rp], [("gp", b, b + 1)])
+            V(GATHER, lambda q, b=b, rb=rb: q.tensor_tensor(T.z[:, b:4 * C:4], at("fh", b).indirect(T[rb][:]), at("gp", b), A.add),
+              [("fh", b, b + 1), rb, ("gp", b, b + 1)], [("z", b, b + 1)])
+        V(0.37, lambda q: q.quantize_mx(T.zq[:], T.zp[:], T.z[:]), ["z"], ["zq", "zp"])
+        Y = "x%d" % (r + 1)
+        for b in range(4):
+            mm("pw", b, "wq", "wp", 128 * b, "zq", "zp", b)
+            S(ROW, lambda q, b=b: copy(q, at("h", b), bank("pw", b), scale=0.03125), [("pw", b, b + 1)], [("h", b, b + 1)])
+            V(GATHER, lambda q, b=b, lb=lb, Y=Y: q.tensor_tensor(T[Y][:, b:4 * C:4], at("h", b).indirect(T[lb][:]), at("fo", b), A.add),
+              [("h", b, b + 1), lb, ("fo", b, b + 1)], [(Y, b, b + 1)])
+    xq, xp, X = "xq%d" % ROUNDS, "xp%d" % ROUNDS, "x%d" % ROUNDS
+    V(0.37, lambda q, xq=xq, xp=xp, X=X: q.quantize_mx(T[xq][:], T[xp][:], T[X][:]), [X], [xq, xp])
+    task(P, "y", 0.07, lambda q: q.dma_start(T.oc[:], T[xq][:].bitcast(dt.uint8)), [xq], [], "dma", "st", 16)
+    for k in range(4):
+        task(P, "y" if k % 2 else "s", 0.07, lambda q, k=k: q.dma_start(T.osc[4 * k:4 * k + 4, :], T[xp][32 * k:32 * k + 4, :]), [xp], [], "dma", "st", 16)
+    mm("pw", 0, "vq", "vp", 0, xq, xp, 0)
+    V(ROW, lambda q: q.tensor_copy(T.eh[:], bank("pw", 0)), [("pw", 0, 1)], ["eh"])
+    task(P, "y", 0.07, lambda q: q.dma_start(T.y[:], T.eh[:]), ["eh"], [], "dma", "st", 16)
+    return sent[0]
+
+
+def rank_program(g, core, T, topo):
+    if T.rank_of(core) is None:
+        return
+    P = new_plan()
+    sent = build(P, g, core, T, topo)
+    order, start, end = schedule(P)
+    count = issue(P, order, start, g, T)
+    g.sync.wait_ge(T.sem.st, 16 * sum(1 for t in P["tasks"] if t["sem"] == "st"))
+    for s, k in sorted(count.items()):
+        g.sync.wait_ge(T.sem[s], k)
+    g.wait_ge(T.sem.snd, sent)

@@ -5,7 +5,7 @@ C = 320
 BANK = 512
 ROUNDS = 3
 BIG = 1e29
-GROUPS = [[6, 5], [4, 3], [2, 1], [0, -1]]
+GROUPS = [[6, 5, 4], [3, 2, 1], [0, -1]]
 
 SCRATCH = {
     "x0": ("sbuf", [128, 4 * C], "bfloat16"), "ut": ("sbuf", [128, 512], "bfloat16"), "vt": ("sbuf", [128, 512], "bfloat16"),
@@ -23,13 +23,14 @@ SCRATCH = {
     "ui": ("sbuf", [128, 8], "int32"), "uo": ("sbuf", [128, 8], "uint16"),
     "mt16": ("sbuf", [128, 20], "uint16"), "lo16": ("sbuf", [128, 20], "uint16"), "hi16": ("sbuf", [128, 20], "uint16"),
     "srow": ("sbuf", [128, C], "float32"), "sm": ("sbuf", [128, C], "float32"),
+    "pr": ("sbuf", [128, C], "bfloat16"), "pws": ("sbuf", [128, C], "float16"),
     "d0": ("sbuf", [128, C], "float32"), "d1": ("sbuf", [128, C], "float32"),
     "cb": ("sbuf", [128, C], "bfloat16"), "cs": ("sbuf", [128, C], "bfloat16"),
     "pb": ("sbuf", [128, C], "bfloat16"), "psn": ("sbuf", [128, C], "bfloat16"),
     "fb": ("sbuf", [128, C], "bfloat16"), "fsn": ("sbuf", [128, C], "bfloat16"),
     "o0": ("sbuf", [128, 20], "uint16"), "o1": ("sbuf", [128, 20], "uint16"), "o3": ("sbuf", [128, 20], "uint16"),
     "er": ("sbuf", [128, C], "float32"), "eh": ("sbuf", [128, C], "float32"), "sw": ("sbuf", [128, C], "bfloat16"),
-    "scn": ("sbuf", [128, C], "float32"), "swn": ("sbuf", [128, C], "float32"), "fmn": ("sbuf", [128, C], "float32"), "fmr": ("sbuf", [128, C], "bfloat16"),
+    "scn": ("sbuf", [128, C], "float16"), "swn": ("sbuf", [128, C], "float16"), "fmn": ("sbuf", [128, C], "float16"), "fmr": ("sbuf", [128, C], "bfloat16"),
     "fo": ("sbuf", [128, 4 * C], "bfloat16"), "fh": ("sbuf", [128, 4 * C], "bfloat16"), "gp": ("sbuf", [128, 4 * C], "bfloat16"),
     "z": ("sbuf", [128, 4 * C], "bfloat16"), "zq": ("sbuf", [128, C], "float8_e4m3fn_x4"), "zp": ("sbuf", [128, C], "uint8"),
     "h": ("sbuf", [128, 4 * C], "bfloat16"),
@@ -43,10 +44,9 @@ for _i, _l in enumerate(GROUPS):
     for _j, _k in enumerate(_l):
         TABLES[_k] = "m%d" % _k if _k >= 0 else "ml"
         SCRATCH[TABLES[_k]] = ("sbuf", [128, C * 2 ** _j], "float32")
-SCRATCH["pn"] = ("sbuf", [128, C * 2 ** (len(GROUPS[-1]) - 1)], "bfloat16")
+LAST = "p%d" % (len(GROUPS) - 1)
 for _k in range(7):
     SCRATCH["l%d" % _k] = ("sbuf", [128, 20], "uint16")
-    SCRATCH["F%d" % _k] = ("sbuf", [128, C], "bfloat16")
 for _r in range(ROUNDS + 1):
     if _r:
         SCRATCH["x%d" % _r] = ("sbuf", [128, 4 * C], "bfloat16")
@@ -246,15 +246,15 @@ def build(P, g, core, T, topo):
     V(0.3, lambda q: q.memset(T.one[:], 1.0), [], ["one"])
     K(1.1, lambda q: q.affine_select(T.big[:], T.one[:], [[-1, 528]], A.is_equal, 0.0, 3, 4), ["one"], ["big"])
     V(ROW, lambda q: q.tensor_scalar(T.dg[:], T.ji[:], 15, None, A.bitwise_and), ["ji"], ["dg"])
-    V(ROW, lambda q: q.tensor_scalar(T.t1[:], T.dg[:], 1.0, 65535.0, A.is_equal, A.mult), ["dg"], ["t1"])
-    V(ROW, lambda q: q.tensor_scalar(T.t2[:], T.dg[:], 0.0, None, A.not_equal), ["dg"], ["t2"])
+    V(ROW, lambda q: q.tensor_scalar(T.t1[:], T.dg[:], 1.0, 320.0, A.is_equal, A.mult), ["dg"], ["t1"])
+    V(ROW, lambda q: q.tensor_scalar(T.t2[:], T.dg[:], 0.0, -16384.0, A.is_equal, A.mult), ["dg"], ["t2"])
     V(2 * ROW, lambda q: q.tensor_tensor(T.wt[:], T.t1[:], T.t2[:], A.add), ["t1", "t2"], ["wt"])
     V(ROW, lambda q: q.tensor_scalar(T.mask[:], T.dg[:], 0.0, None, A.is_equal), ["dg"], ["mask"])
     V(ROW, lambda q: q.tensor_scalar(T.cap[:], T.mask[:], 2 * BIG, -BIG, A.mult, A.add), ["mask"], ["cap"])
     V(ROW, lambda q: q.tensor_scalar(T.rs[:], T.rs0[:], 1.0, None, A.min), ["rs0"], ["rs"])
     V(SMALL, lambda q: q.tensor_scalar(T.pa15[:], T.pi[:], 15, None, A.bitwise_and), ["pi"], ["pa15"])
-    V(SMALL, lambda q: q.tensor_scalar(L("f0"), T.pa15[:], 15.0, 1.0 - 2.0 ** -16, A.is_equal, A.mult), ["pa15"], ["f0"])
-    V(SMALL, lambda q: q.tensor_scalar(L("col"), L("f0"), 2.0 ** -16, None, A.add), ["f0"], ["col"])
+    V(SMALL, lambda q: q.tensor_scalar(L("f0"), T.pa15[:], 15.0, 320.0, A.is_equal, A.mult), ["pa15"], ["f0"])
+    V(SMALL, lambda q: q.tensor_scalar(L("col"), L("f0"), -160.0, None, A.add), ["f0"], ["col"])
     V(SMALL, lambda q: q.tensor_tensor(L("cw"), T.pa15[:], T.ci[:], A.add), ["pa15", "ci"], ["cw"])
     V(SMALL, lambda q: q.tensor_scalar(L("cwc"), L("cw"), -160.0, None, A.add), ["cw"], ["cwc"])
     V(SMALL, lambda q: q.tensor_scalar(L("cwu"), L("cw"), 1.0 / C, None, A.mult), ["cw"], ["cwu"])
@@ -271,6 +271,7 @@ def build(P, g, core, T, topo):
     V(0.16, lambda q: q.quantize_mx(T.vq[:], T.vp[:], T.vt[:]), ["vt"], ["vq", "vp"])
 
     V(SMALL, lambda q: q.tensor_copy(T.l0[:], T.nxi[:]), ["nxi"], ["l0"])
+    V(SMALL, lambda q: q.tensor_copy(L("fw"), T.nxi[:]), ["nxi"], ["fw"])
     V(SMALL, lambda q: q.tensor_copy(T.mt16[:], T.mti[:]), ["mti"], ["mt16"])
     V(SMALL, lambda q: q.tensor_copy(L("bd"), T.mti[:]), ["mti"], ["bd"])
     V(SMALL, lambda q: q.tensor_tensor(L("be"), L("bd"), L("cw"), A.min), ["bd", "cw"], ["be"])
@@ -284,31 +285,31 @@ def build(P, g, core, T, topo):
     def masked(dst, win, i, k, off):
         V(GATHER, lambda q: q.tensor_tensor(T[dst][:], T[win][:, C * i:C * k].indirect(T[off][:]), T.mask[:], A.mult), [(win, i, k), off, "mask"], [dst])
 
+    def look(dst, win, k, off):
+        S(GATHER, lambda q: copy(q, T[dst][:], T[win][:, 0:C * k].indirect(T[off][:])), [(win, 0, k), off], [dst])
+
     def running(dst, src):
         V(SCAN2, lambda q: q.tensor_tensor_scan(T[dst][:], T.rs[:], T[src][:], 0.0, A.mult, A.add), ["rs", src], [dst])
 
-    def weighted(dst, src):
-        V(SCAN4, lambda q: q.tensor_tensor_scan(T[dst][:], T.wt[:], T[src][:], 0.0, A.mult, A.add), ["wt", src], [dst])
+    def weighted(dst, src, a=0):
+        V(SCAN2, lambda q: q.tensor_tensor_scan(T[dst][:], T.wt[:], at(src, a), 0.0, A.add, A.max), ["wt", (src, a, a + 1)], [dst])
 
-    def powers(first):
-        row("F0", 0, "idr", 0, 0)
+    def at_f(k):
+        return [("p%d" % i, 2 ** levels.index(k)) for i, levels in enumerate(GROUPS) if k in levels][0]
+
+    def powers():
+        row(*at_f(0), "idr", 0, 0)
         for k in range(6):
-            b, l = "F%d" % (k + 1), "l%d" % (k + 1)
-            if first:
-                masked("pb", "F%d" % k, 0, 1, "l%d" % k)
-                running("psn", "pb")
-                V(SMALL, lambda q, l=l: q.tensor_scalar(T[l][:], every16("psn"), 160.0, None, A.add), ["psn"], [l])
-            row(b, 0, "F%d" % k, 0, k)
-            if not first:
-                weighted("scn", b)
-                V(SMALL, lambda q, l=l: q.tensor_scalar(T[l][:], every16("scn"), col, 160.25, A.mult, A.add), ["scn", "col"], [l])
+            l = "l%d" % (k + 1)
+            row(*at_f(k + 1), *at_f(k), k)
+            weighted("scn", *at_f(k + 1))
+            V(SMALL, lambda q, l=l: q.tensor_scalar(T[l][:], every16("scn"), col, None, A.add), ["scn", "col"], [l])
+        b, a = at_f(1)
+        S(ROW, lambda q: copy(q, at(LAST, 2), at(b, a)), [(b, a, a + 1)], [(LAST, 2, 3)])
         for i, levels in enumerate(GROUPS):
             for j, k in enumerate(levels):
-                if k >= 0:
-                    for a in range(2 ** j):
-                        row("p%d" % i, 2 ** j + a, "p%d" % i, a, k)
-        for a in range(2 ** (len(GROUPS[-1]) - 1)):
-            row("pn", a, "p%d" % (len(GROUPS) - 1), a, 0)
+                for a2 in range(1, 2 ** j if k >= 0 else 0):
+                    row("p%d" % i, 2 ** j + a2, "p%d" % i, a2, k)
 
     sent = [0]
 
@@ -333,7 +334,7 @@ def build(P, g, core, T, topo):
     def bank(out, b):
         return T[out][:, BANK * b:BANK * b + C]
 
-    powers(False)
+    powers()
     for r in range(ROUNDS):
         X, xq, xp, aq, ap = "x%d" % r, "xq%d" % r, "xp%d" % r, "aq%d" % r, "ap%d" % r
         lp, lb, rp, rb = "lp%d" % r, "lb%d" % r, "rp%d" % r, "rb%d" % r
@@ -346,11 +347,12 @@ def build(P, g, core, T, topo):
         V(GATHER, lambda q: q.tensor_copy(at("m0", 0), T.srow[:].indirect(T.l0[:])), ["srow", "l0"], [("m0", 0, 1)])
         S(GATHER, lambda q: copy(q, at("ml", 0), T.srow[:].indirect(T.l0[:])), ["srow", "l0"], [("ml", 0, 1)])
         for k in range(6):
-            twin = "d%d" % (k % 2) if k else "ml"
-            if k:
-                V(ROW, lambda q, k=k, twin=twin: q.tensor_copy(at(twin, 0), at("m%d" % k, 0)), [("m%d" % k, 0, 1)], [(twin, 0, 1)])
-            V(GATHER, lambda q, k=k, twin=twin: q.tensor_tensor(at("m%d" % (k + 1), 0), at("m%d" % k, 0).indirect(T["l%d" % k][:]), at(twin, 0), A.max),
-              [("m%d" % k, 0, 1), (twin, 0, 1), "l%d" % k], [("m%d" % (k + 1), 0, 1)])
+            twin, m0, m1 = ("d%d" % (k % 2) if k else "ml"), "m%d" % k, "m%d" % (k + 1)
+            V(GATHER, lambda q, k=k, twin=twin, m0=m0, m1=m1: q.tensor_tensor(at(m1, 0), at(m0, 0).indirect(T["l%d" % k][:]), at(twin, 0), A.max),
+              [(m0, 0, 1), (twin, 0, 1), "l%d" % k], [(m1, 0, 1)])
+            if k < 5:
+                d = "d%d" % ((k + 1) % 2)
+                S(ROW, lambda q, d=d, m1=m1: copy(q, at(d, 0), at(m1, 0)), [(m1, 0, 1)], [(d, 0, 1)])
         for levels in GROUPS:
             for i, k in enumerate(levels):
                 for j in range(i):
@@ -377,20 +379,20 @@ def build(P, g, core, T, topo):
                 V(SMALL, lambda q, f=f, off=off, j=j: q.tensor_scalar(T[off][:], L(f), float(C * 2 ** j), 0.25, A.mult, A.add), [f], [off])
                 if j + 1 < len(levels) and levels[j + 1] >= 0:
                     place = "h%d" % (j % 2)
-                    S(0.1, lambda q, f=f, place=place: copy(q, L(place), L(f), scale=0.5), [f], [place])
+                    V(SMALL, lambda q, f=f, place=place: q.tensor_scalar(L(place), L(f), 0.5, None, A.mult), [f], [place])
                 if j + 1 < len(levels) and levels[j + 1] < 0:
-                    masked("pb", "p%d" % i, 0, 2 ** (j + 1), off)
-                    running("psn", "pb")
-                    V(SMALL, lambda q, lp=lp: q.tensor_scalar(T[lp][:], every16("psn"), 160.0, None, A.add), ["psn"], [lp])
+                    look("pr", "p%d" % i, 2 ** (j + 1), off)
+                    weighted("pws", "pr")
+                    V(SMALL, lambda q, lp=lp: q.tensor_scalar(T[lp][:], every16("pws"), col, None, A.add), ["pws", "col"], [lp])
                     send(r, [(T[rp][:], T[lp][:], lp)], "arp%d" % r, [rp], 2.6)
-                    masked("fb", "pn", 0, 2 ** (j + 1), off)
+                    masked("fb", LAST, 1, 3, off)
                     running("fsn", "fb")
                     V(SMALL, lambda q: q.tensor_tensor(L("bd"), L("cwc"), every16("fsn"), A.subtract), ["cwc", "fsn"], ["bd"])
             if not last:
                 masked("pb", "p%d" % i, 0, 2 ** len(levels), off)
                 running("psn", "pb")
                 V(SMALL, lambda q: q.tensor_scalar(T.o3[:], every16("psn"), 160.0, None, A.add), ["psn"], ["o3"])
-                S(0.1, lambda q: copy(q, L("pif"), every16("psn"), scale=1.0 / C, bias=160.0 / C), ["psn"], ["pif"])
+                V(SMALL, lambda q: q.tensor_scalar(L("pif"), every16("psn"), 1.0 / C, 160.0 / C, A.mult, A.add), ["psn"], ["pif"])
         V(SMALL, lambda q: q.tensor_tensor(L("be"), L("bd"), every16("cs"), A.mult), ["bd", "cs"], ["be"])
         V(SMALL, lambda q: q.tensor_tensor(L("bf"), L("be"), every16("fsn"), A.add), ["be", "fsn"], ["bf"])
         V(SMALL, lambda q, lb=lb: q.tensor_scalar(T[lb][:], L("bf"), 160.0, None, A.add), ["bf"], [lb])
@@ -399,17 +401,17 @@ def build(P, g, core, T, topo):
         S(GATHER, lambda q: copy(q, T.eh[:], T.er[:].indirect(T.hi16[:])), ["er", "hi16"], ["eh"])
         V(GATHER, lambda q: q.tensor_tensor(T.sw[:], T.er[:].indirect(T.lo16[:]), T.eh[:], A.is_gt), ["er", "eh", "lo16"], ["sw"])
         weighted("swn", "sw")
-        V(SMALL, lambda q: q.tensor_scalar(L("swc"), every16("swn"), col, 0.5, A.mult, A.is_ge), ["swn", "col"], ["swc"])
-        S(GATHER, lambda q: copy(q, T.fmr[:], T.F0[:].indirect(T.mt16[:])), ["F0", "mt16"], ["fmr"])
+        V(SMALL, lambda q: q.tensor_scalar(L("swc"), every16("swn"), col, -160.0, A.add, A.add), ["swn", "col"], ["swc"])
+        S(GATHER, lambda q: copy(q, T.fmr[:], at(*at_f(0)).indirect(T.mt16[:])), [at_f(0) + (at_f(0)[1] + 1,), "mt16"], ["fmr"])
         weighted("fmn", "fmr")
-        V(SMALL, lambda q: q.tensor_scalar(L("fmv"), every16("fmn"), col, 160.0, A.mult, A.add), ["fmn", "col"], ["fmv"])
-        V(SMALL, lambda q: q.tensor_copy(L("fw"), T.l0[:]), ["l0"], ["fw"])
-        V(SMALL, lambda q: q.tensor_tensor(L("fd"), L("fmv"), L("fw"), A.subtract), ["fmv", "fw"], ["fd"])
+        V(SMALL, lambda q: q.tensor_scalar(L("fmv"), every16("fmn"), col, None, A.add), ["fmn", "col"], ["fmv"])
+        fw, fn = ("fw", "fn") if r % 2 == 0 else ("fn", "fw")
+        V(SMALL, lambda q, fw=fw: q.tensor_tensor(L("fd"), L("fmv"), L(fw), A.subtract), ["fmv", fw], ["fd"])
         V(SMALL, lambda q: q.tensor_tensor(L("fe"), L("fd"), L("swc"), A.mult), ["fd", "swc"], ["fe"])
-        V(SMALL, lambda q: q.tensor_tensor(L("fn"), L("fw"), L("fe"), A.add), ["fw", "fe"], ["fn"])
-        V(SMALL, lambda q: q.tensor_scalar(T.l0[:], L("fn"), 0.25, None, A.add), ["fn"], ["l0"])
+        V(SMALL, lambda q, fw=fw, fn=fn: q.tensor_tensor(L(fn), L(fw), L("fe"), A.add), [fw, "fe"], [fn])
+        V(SMALL, lambda q, fn=fn: q.tensor_copy(T.l0[:], L(fn)), [fn], ["l0"])
         if r < ROUNDS - 1:
-            powers(False)
+            powers()
         else:
             S(GATHER, lambda q: copy(q, T.er[:], T.idr[:].indirect(T.l0[:]), bias=160.0), ["idr", "l0"], ["er"])
             task(P, "y", 0.07, lambda q: q.dma_start(T.nf[:], T.er[0:128:16, :]), ["er"], [], "dma", "st", 16)

@@ -1,3 +1,4 @@
+import numpy as np
 from concourse.mybir import dt, AluOpType, ActivationFunctionType
 A = AluOpType
 AF = ActivationFunctionType
@@ -5,7 +6,7 @@ C = 320
 BANK = 512
 ROUNDS = 3
 BIG = 1e29
-GROUPS = [[6, 5, 4], [3, 2, 1], [0, -1]]
+GROUPS = [[6, 5], [4, 3], [2, 1], [0, -1]]
 
 SCRATCH = {
     "x0": ("sbuf", [128, 4 * C], "bfloat16"), "ut": ("sbuf", [128, 512], "bfloat16"), "vt": ("sbuf", [128, 512], "bfloat16"),
@@ -26,8 +27,9 @@ SCRATCH = {
     "pr": ("sbuf", [128, C], "bfloat16"), "pws": ("sbuf", [128, C], "float16"),
     "d0": ("sbuf", [128, C], "float32"), "d1": ("sbuf", [128, C], "float32"),
     "cb": ("sbuf", [128, C], "bfloat16"), "cs": ("sbuf", [128, C], "bfloat16"),
-    "pb": ("sbuf", [128, C], "bfloat16"), "psn": ("sbuf", [128, C], "bfloat16"),
-    "fb": ("sbuf", [128, C], "bfloat16"), "fsn": ("sbuf", [128, C], "bfloat16"),
+    "pb": ("sbuf", [128, C], "bfloat16"), "psn": ("sbuf", [128, C], "float16"),
+    "fb": ("sbuf", [128, C], "bfloat16"), "fr": ("sbuf", [128, C], "bfloat16"), "fsn": ("sbuf", [128, C], "float16"),
+    "fs": ("sbuf", [128, C], "bfloat16"),
     "o0": ("sbuf", [128, 20], "uint16"), "o1": ("sbuf", [128, 20], "uint16"), "o3": ("sbuf", [128, 20], "uint16"),
     "er": ("sbuf", [128, C], "float32"), "eh": ("sbuf", [128, C], "float32"), "sw": ("sbuf", [128, C], "bfloat16"),
     "scn": ("sbuf", [128, C], "float16"), "swn": ("sbuf", [128, C], "float16"), "fmn": ("sbuf", [128, C], "float16"), "fmr": ("sbuf", [128, C], "bfloat16"),
@@ -36,14 +38,15 @@ SCRATCH = {
     "h": ("sbuf", [128, 4 * C], "bfloat16"),
     "pu": ("psum", [128, 2048], "float32"), "pw": ("psum", [128, 2048], "float32"),
 }
-LISTS = ["cw", "cwc", "cwu", "col", "f0", "f1", "h0", "h1", "pif", "bd", "be", "bf", "swc", "fmv", "fw", "fd", "fe", "fn"]
+LISTS = ["cw", "cwu", "col", "f0", "f1", "h0", "h1", "pif", "bd", "be", "bf", "swc", "fmv", "fw", "fd", "fe", "fn", "fv"]
 SCRATCH["sml"] = ("sbuf", [128, 20 * len(LISTS)], "float32")
-TABLES = {}
+TABLES, PASSED = {}, {}
 for _i, _l in enumerate(GROUPS):
     SCRATCH["p%d" % _i] = ("sbuf", [128, C * 2 ** len(_l)], "bfloat16")
     for _j, _k in enumerate(_l):
         TABLES[_k] = "m%d" % _k if _k >= 0 else "ml"
-        SCRATCH[TABLES[_k]] = ("sbuf", [128, C * 2 ** _j], "float32")
+        PASSED[_k] = _l[:_j] if _j else GROUPS[_i - 1] if _i else []
+        SCRATCH[TABLES[_k]] = ("sbuf", [128, C * 2 ** len(PASSED[_k])], "float32")
 LAST = "p%d" % (len(GROUPS) - 1)
 for _k in range(7):
     SCRATCH["l%d" % _k] = ("sbuf", [128, 20], "uint16")
@@ -62,7 +65,8 @@ SEMAPHORES += ["%s%d" % (_n, _r) for _n in ("ax", "arp", "arb") for _r in range(
 SEMAPHORES += ["ld_" + _n for _n in ("x", "u", "v", "nx", "mt", "wc", "ws")]
 
 GATHER, SCAN2, SCAN4, ROW, SMALL = 0.58, 0.17, 0.33, 0.34, 0.08
-HOP, SAME = 0.12, 0.06
+HOP, SAME = 0.2, 0.1
+SHARED = {}
 
 
 def new_plan():
@@ -73,7 +77,7 @@ def overlap(a, b):
     return a[0] < b[1] and b[0] < a[1]
 
 
-def task(P, eng, dur, fn, reads, writes, kind="op", sem=None, inc=1, after=()):
+def task(P, eng, dur, fn, reads, writes, kind="op", sem=None, inc=1, after=(), behind=()):
     def reg(x):
         return (x, 0, 1 << 20) if isinstance(x, str) else x
     n = len(P["tasks"])
@@ -102,47 +106,66 @@ def task(P, eng, dur, fn, reads, writes, kind="op", sem=None, inc=1, after=()):
     for b, lo, hi in rd:
         P["r"].setdefault(b, []).append((lo, hi, n))
     deps.pop(n, None)
+    for a in behind:
+        deps.setdefault(a, False)
     P["tasks"].append({"eng": eng, "dur": dur, "fn": fn, "deps": deps, "kind": kind, "sem": sem, "inc": inc})
     return n
 
 
-def schedule(P):
+def schedule(P, tries=5000):
     ts = P["tasks"]
     n = len(ts)
+    lags = [[(d, HOP if ts[d]["eng"] != t["eng"] else SAME if t["deps"][d] else 0.0) for d in t["deps"]] for t in ts]
     succ = [[] for _ in range(n)]
-    for i, t in enumerate(ts):
-        for d in t["deps"]:
+    for i in range(n):
+        for d, _ in lags[i]:
             succ[d].append(i)
-
-    def lag(d, i):
-        return SAME if ts[d]["eng"] == ts[i]["eng"] else HOP
-    up = [0.0] * n
+    up = [t["dur"] for t in ts]
     for i in range(n - 1, -1, -1):
-        up[i] = ts[i]["dur"] + max([up[s] + lag(i, s) for s in succ[i]] or [0.0])
-    left = [len(t["deps"]) for t in ts]
-    ready = [i for i in range(n) if left[i] == 0]
-    slots = {}
-    start, end = [0.0] * n, [0.0] * n
-    while ready:
-        i = max(ready, key=lambda k: (up[k], -k))
-        ready.remove(i)
-        t = ts[i]
-        at = max([end[d] + lag(d, i) for d in t["deps"]] or [0.0])
-        if t["eng"] != "net":
-            line = slots.setdefault(t["eng"], [])
-            k = 0
-            for k in range(len(line) + 1):
-                s = max(at, line[k - 1][1] if k else 0.0)
-                if k == len(line) or s + t["dur"] <= line[k][0] + 1e-9:
-                    break
-            line.insert(k, (s, s + t["dur"], i))
-            at = s
-        start[i], end[i] = at, at + t["dur"]
-        for s in succ[i]:
-            left[s] -= 1
-            if left[s] == 0:
-                ready.append(s)
-    return {e: [x[2] for x in line] for e, line in slots.items()}, start, end
+        for d, lag in lags[i]:
+            up[d] = max(up[d], ts[d]["dur"] + lag + up[i])
+
+    def place(rank):
+        left = [len(x) for x in lags]
+        ready = [i for i in range(n) if left[i] == 0]
+        slots = {}
+        start, end = [0.0] * n, [0.0] * n
+        while ready:
+            i = max(ready, key=lambda k: rank[k])
+            ready.remove(i)
+            t = ts[i]
+            at, dur = 0.0, t["dur"]
+            for d, lag in lags[i]:
+                at = max(at, end[d] + lag)
+            if t["eng"] != "net":
+                line = slots.setdefault(t["eng"], [])
+                k = len(line)
+                while k and line[k - 1][1] > at:
+                    k -= 1
+                while True:
+                    s = max(at, line[k - 1][1] if k else 0.0)
+                    if k == len(line) or s + dur <= line[k][0] + 1e-9:
+                        break
+                    k += 1
+                line.insert(k, (s, s + dur, i))
+                at = s
+            start[i], end[i] = at, at + dur
+            for s in succ[i]:
+                left[s] -= 1
+                if left[s] == 0:
+                    ready.append(s)
+        return max(end), {e: [x[2] for x in line] for e, line in slots.items()}, start
+    best, rank = place(up), up
+    rng = np.random.default_rng(7)
+    for _ in range(tries):
+        at, width = rng.random() * max(up), [2, 5, 10][rng.integers(3)]
+        part, step = [0.05, 0.15, 0.4][rng.integers(3)], [0.5, 1.5, 4.0][rng.integers(3)]
+        hit, by = rng.random(n) < part, rng.standard_normal(n) * step
+        trial = [float(rank[i] + by[i]) if hit[i] and abs(up[i] - at) < width else rank[i] for i in range(n)]
+        got = place(trial)
+        if got[0] <= best[0]:
+            best, rank = got, trial
+    return best[1], best[2], best[0]
 
 
 def issue(P, order, start, g, T):
@@ -204,8 +227,8 @@ def build(P, g, core, T, topo):
     def L(name):
         return lists[name]
 
-    def V(dur, fn, reads, writes):
-        return task(P, "v", dur, fn, reads, writes)
+    def V(dur, fn, reads, writes, behind=()):
+        return task(P, "v", dur, fn, reads, writes, behind=behind)
 
     def S(dur, fn, reads, writes):
         return task(P, "s", dur, fn, reads, writes)
@@ -256,7 +279,6 @@ def build(P, g, core, T, topo):
     V(SMALL, lambda q: q.tensor_scalar(L("f0"), T.pa15[:], 15.0, 320.0, A.is_equal, A.mult), ["pa15"], ["f0"])
     V(SMALL, lambda q: q.tensor_scalar(L("col"), L("f0"), -160.0, None, A.add), ["f0"], ["col"])
     V(SMALL, lambda q: q.tensor_tensor(L("cw"), T.pa15[:], T.ci[:], A.add), ["pa15", "ci"], ["cw"])
-    V(SMALL, lambda q: q.tensor_scalar(L("cwc"), L("cw"), -160.0, None, A.add), ["cw"], ["cwc"])
     V(SMALL, lambda q: q.tensor_scalar(L("cwu"), L("cw"), 1.0 / C, None, A.mult), ["cw"], ["cwu"])
     V(SMALL, lambda q: q.tensor_copy(T.uo[:], T.ui[:]), ["ui"], ["uo"])
     for i in range(len(GROUPS)):
@@ -282,11 +304,8 @@ def build(P, g, core, T, topo):
     def row(out, a, win, i, k):
         S(GATHER, lambda q: copy(q, at(out, a), at(win, i).indirect(T["l%d" % k][:])), [(win, i, i + 1), "l%d" % k], [(out, a, a + 1)])
 
-    def masked(dst, win, i, k, off):
-        V(GATHER, lambda q: q.tensor_tensor(T[dst][:], T[win][:, C * i:C * k].indirect(T[off][:]), T.mask[:], A.mult), [(win, i, k), off, "mask"], [dst])
-
-    def look(dst, win, k, off):
-        S(GATHER, lambda q: copy(q, T[dst][:], T[win][:, 0:C * k].indirect(T[off][:])), [(win, 0, k), off], [dst])
+    def look(dst, win, i, k, off):
+        S(GATHER, lambda q: copy(q, T[dst][:], T[win][:, C * i:C * k].indirect(T[off][:])), [(win, i, k), off], [dst])
 
     def running(dst, src):
         V(SCAN2, lambda q: q.tensor_tensor_scan(T[dst][:], T.rs[:], T[src][:], 0.0, A.mult, A.add), ["rs", src], [dst])
@@ -323,9 +342,9 @@ def build(P, g, core, T, topo):
             sent[0] += len(topo.engines(core, dst))
         return task(P, "net", latency, None, [], land, "land", sem, len(topo.engines(src, core)) * len(pairs), after=ids)
 
-    def compare(level, off):
+    def compare(level, off, behind=()):
         win = TABLES[level]
-        V(GATHER, lambda q: q.tensor_tensor(T.cb[:], T[win][:].indirect(T[off][:]), T.sm[:], A.is_le), [win, off, "sm"], ["cb"])
+        V(GATHER, lambda q: q.tensor_tensor(T.cb[:], T[win][:].indirect(T[off][:]), T.sm[:], A.is_le), [win, off, "sm"], ["cb"], behind)
 
     def mm(out, b, wq, wp, a, xq, xp, unit):
         E(0.35, lambda q: q.matmul_mx(T[out][:, BANK * b:BANK * b + C], T[wq][:, a:a + 128], T[wp][:, a:a + 128], T[xq][:], T[xp][:], True, True),
@@ -346,56 +365,62 @@ def build(P, g, core, T, topo):
         V(ROW, lambda q: q.tensor_tensor(T.sm[:], bank("pw", 1), T.cap[:], A.min), [("pw", 1, 2), "cap"], ["sm"])
         V(GATHER, lambda q: q.tensor_copy(at("m0", 0), T.srow[:].indirect(T.l0[:])), ["srow", "l0"], [("m0", 0, 1)])
         S(GATHER, lambda q: copy(q, at("ml", 0), T.srow[:].indirect(T.l0[:])), ["srow", "l0"], [("ml", 0, 1)])
-        for k in range(6):
+        for k in range(5):
             twin, m0, m1 = ("d%d" % (k % 2) if k else "ml"), "m%d" % k, "m%d" % (k + 1)
             V(GATHER, lambda q, k=k, twin=twin, m0=m0, m1=m1: q.tensor_tensor(at(m1, 0), at(m0, 0).indirect(T["l%d" % k][:]), at(twin, 0), A.max),
               [(m0, 0, 1), (twin, 0, 1), "l%d" % k], [(m1, 0, 1)])
-            if k < 5:
+            if k < 4:
                 d = "d%d" % ((k + 1) % 2)
                 S(ROW, lambda q, d=d, m1=m1: copy(q, at(d, 0), at(m1, 0)), [(m1, 0, 1)], [(d, 0, 1)])
-        for levels in GROUPS:
-            for i, k in enumerate(levels):
-                for j in range(i):
-                    for a in range(2 ** j):
-                        row(TABLES[k], 2 ** j + a, TABLES[k], a, levels[j])
+        for k, passed in PASSED.items():
+            for j, l in enumerate(passed):
+                for a in range(2 ** j):
+                    row(TABLES[k], 2 ** j + a, TABLES[k], a, l)
         for b in range(4):
             mm("pu", b, "eq", "ep", 128 * b, xq, xp, b)
-            S(ROW, lambda q, b=b: copy(q, at("fo", b), bank("pu", b)), [("pu", b, b + 1)], [("fo", b, b + 1)])
+            (V if b < 2 else S)(ROW, lambda q, b=b: (q.tensor_copy if b < 2 else lambda o, i: copy(q, o, i))(at("fo", b), bank("pu", b)),
+                                [("pu", b, b + 1)], [("fo", b, b + 1)])
         for b in range(4):
             mm("pu", b, "eq", "ep", 128 * b, aq, ap, b)
             S(ROW, lambda q, b=b: copy(q, at("fh", b), bank("pu", b), scale=0.5), [("pu", b, b + 1)], [("fh", b, b + 1)])
         for i, levels in enumerate(GROUPS):
-            place, off, last = "cwu" if i == 0 else "pif", "o3", i == len(GROUPS) - 1
+            place, last = "cwu" if i == 0 else "pif", i == len(GROUPS) - 1
             for j, k in enumerate(levels):
                 if i == 0 and j == 0:
-                    V(2 * ROW, lambda q: q.tensor_tensor(T.cb[:], at("m6", 0), T.sm[:], A.is_le), [("m6", 0, 1), "sm"], ["cb"])
+                    V(2 * ROW, lambda q: q.tensor_tensor(T.fb[:], at("m5", 0), T.sm[:], A.is_le), [("m5", 0, 1), "sm"], ["fb"])
+                    running("fs", "fb")
+                    V(GATHER, lambda q: q.tensor_tensor(T.cb[:], at("m5", 0).indirect(T.l5[:]), T.sm[:], A.is_le), [("m5", 0, 1), "l5", "sm"], ["cb"])
+                    running("cs", "cb")
+                    V(SMALL, lambda q: q.tensor_tensor(L("fv"), every16("cs"), every16("fs"), A.mult), ["cs", "fs"], ["fv"])
                 else:
-                    compare(k, off)
-                running("cs", "cb")
+                    compare(k, off, behind)
+                    running("cs", "cb")
+                behind = []
                 if k < 0:
                     break
                 f, off = "f%d" % (j % 2), "o%d" % (j % 2)
-                V(SMALL, lambda q, f=f, place=place: q.tensor_tensor(L(f), L(place), every16("cs"), A.add), [place, "cs"], [f])
+                V(SMALL, lambda q, f=f, place=place, top=i + j == 0: q.tensor_tensor(L(f), L(place), L("fv") if top else every16("cs"), A.add),
+                  [place, "cs", "fv"] if i + j == 0 else [place, "cs"], [f])
                 V(SMALL, lambda q, f=f, off=off, j=j: q.tensor_scalar(T[off][:], L(f), float(C * 2 ** j), 0.25, A.mult, A.add), [f], [off])
                 if j + 1 < len(levels) and levels[j + 1] >= 0:
                     place = "h%d" % (j % 2)
-                    V(SMALL, lambda q, f=f, place=place: q.tensor_scalar(L(place), L(f), 0.5, None, A.mult), [f], [place])
+                    behind = [V(SMALL, lambda q, f=f, place=place: q.tensor_scalar(L(place), L(f), 0.5, None, A.mult), [f], [place])]
                 if j + 1 < len(levels) and levels[j + 1] < 0:
-                    look("pr", "p%d" % i, 2 ** (j + 1), off)
+                    look("pr", LAST, 0, 2, off)
+                    look("fr", LAST, 1, 3, off)
                     weighted("pws", "pr")
                     V(SMALL, lambda q, lp=lp: q.tensor_scalar(T[lp][:], every16("pws"), col, None, A.add), ["pws", "col"], [lp])
                     send(r, [(T[rp][:], T[lp][:], lp)], "arp%d" % r, [rp], 2.6)
-                    masked("fb", LAST, 1, 3, off)
-                    running("fsn", "fb")
-                    V(SMALL, lambda q: q.tensor_tensor(L("bd"), L("cwc"), every16("fsn"), A.subtract), ["cwc", "fsn"], ["bd"])
+                    weighted("fsn", "fr")
+                    V(SMALL, lambda q: q.tensor_scalar(L("fv"), every16("fsn"), col, None, A.add), ["fsn", "col"], ["fv"])
+                    V(SMALL, lambda q: q.tensor_tensor(L("bd"), L("cw"), L("fv"), A.subtract), ["cw", "fv"], ["bd"])
             if not last:
-                masked("pb", "p%d" % i, 0, 2 ** len(levels), off)
-                running("psn", "pb")
-                V(SMALL, lambda q: q.tensor_scalar(T.o3[:], every16("psn"), 160.0, None, A.add), ["psn"], ["o3"])
-                V(SMALL, lambda q: q.tensor_scalar(L("pif"), every16("psn"), 1.0 / C, 160.0 / C, A.mult, A.add), ["psn"], ["pif"])
+                look("pb", "p%d" % i, 0, 2 ** len(levels), off)
+                weighted("psn", "pb")
+                V(SMALL, lambda q: q.tensor_scalar(L("pif"), every16("psn"), col, 1.0 / C, A.add, A.mult), ["psn", "col"], ["pif"])
         V(SMALL, lambda q: q.tensor_tensor(L("be"), L("bd"), every16("cs"), A.mult), ["bd", "cs"], ["be"])
-        V(SMALL, lambda q: q.tensor_tensor(L("bf"), L("be"), every16("fsn"), A.add), ["be", "fsn"], ["bf"])
-        V(SMALL, lambda q, lb=lb: q.tensor_scalar(T[lb][:], L("bf"), 160.0, None, A.add), ["bf"], [lb])
+        V(SMALL, lambda q: q.tensor_tensor(L("bf"), L("be"), L("fv"), A.add), ["be", "fv"], ["bf"])
+        V(SMALL, lambda q, lb=lb: q.tensor_copy(T[lb][:], L("bf")), ["bf"], [lb])
         send(r, [(T[rb][:], T[lb][:], lb)], "arb%d" % r, [rb], 2.6)
         S(GATHER, lambda q, lb=lb: copy(q, T.er[:], T.srow[:].indirect(T[lb][:])), ["srow", lb], ["er"])
         S(GATHER, lambda q: copy(q, T.eh[:], T.er[:].indirect(T.hi16[:])), ["er", "hi16"], ["eh"])
@@ -442,7 +467,9 @@ def rank_program(g, core, T, topo):
         return
     P = new_plan()
     sent = build(P, g, core, T, topo)
-    order, start, end = schedule(P)
+    if "order" not in SHARED:
+        SHARED["order"] = schedule(P)
+    order, start, _ = SHARED["order"]
     count = issue(P, order, start, g, T)
     g.sync.wait_ge(T.sem.st, 16 * sum(1 for t in P["tasks"] if t["sem"] == "st"))
     for s, k in sorted(count.items()):

import numpy as np
from concourse.mybir import dt, AluOpType, ActivationFunctionType
A = AluOpType
AF = ActivationFunctionType
C = 320
BANK = 512
ROUNDS = 3
BIG = 1e29
GROUPS = [[6, 5], [4, 3], [2, 1], [0, -1]]

SCRATCH = {
    "x0": ("sbuf", [128, 4 * C], "bfloat16"), "ut": ("sbuf", [128, 512], "bfloat16"), "vt": ("sbuf", [128, 512], "bfloat16"),
    "nxi": ("sbuf", [128, 20], "int32"), "mti": ("sbuf", [128, 20], "int32"),
    "wq": ("sbuf", [128, 512], "float8_e4m3fn_x4"), "wp": ("sbuf", [128, 512], "uint8"),
    "uq": ("sbuf", [128, 128], "float8_e4m3fn_x4"), "up": ("sbuf", [128, 128], "uint8"),
    "uqr": ("sbuf", [128, 128], "float8_e4m3fn_x4"), "upr": ("sbuf", [128, 128], "uint8"),
    "vq": ("sbuf", [128, 128], "float8_e4m3fn_x4"), "vp": ("sbuf", [128, 128], "uint8"),
    "eq": ("sbuf", [128, 512], "float8_e4m3fn_x4"), "ep": ("sbuf", [128, 512], "uint8"),
    "one": ("sbuf", [128, 528], "bfloat16"), "big": ("sbuf", [128, 528], "bfloat16"),
    "ji": ("sbuf", [128, C], "int32"), "dg": ("sbuf", [128, C], "int32"), "t1": ("sbuf", [128, C], "float32"), "t2": ("sbuf", [128, C], "float32"),
    "rs0": ("sbuf", [128, C], "bfloat16"), "rs": ("sbuf", [128, C], "bfloat16"), "wt": ("sbuf", [128, C], "bfloat16"),
    "mask": ("sbuf", [128, C], "bfloat16"), "cap": ("sbuf", [128, C], "float32"), "idr": ("sbuf", [128, C], "bfloat16"),
    "pi": ("sbuf", [128, 20], "int32"), "pa15": ("sbuf", [128, 20], "int32"), "ci": ("sbuf", [128, 20], "int32"),
    "ui": ("sbuf", [128, 8], "int32"), "uo": ("sbuf", [128, 8], "uint16"),
    "mt16": ("sbuf", [128, 20], "uint16"), "lo16": ("sbuf", [128, 20], "uint16"), "hi16": ("sbuf", [128, 20], "uint16"),
    "srow": ("sbuf", [128, C], "float32"), "sm": ("sbuf", [128, C], "float32"),
    "pr": ("sbuf", [128, C], "bfloat16"), "pws": ("sbuf", [128, C], "float16"),
    "d0": ("sbuf", [128, C], "float32"), "d1": ("sbuf", [128, C], "float32"),
    "cb": ("sbuf", [128, C], "bfloat16"), "cs": ("sbuf", [128, C], "bfloat16"),
    "pb": ("sbuf", [128, C], "bfloat16"), "psn": ("sbuf", [128, C], "float16"),
    "fb": ("sbuf", [128, C], "bfloat16"), "fr": ("sbuf", [128, C], "bfloat16"), "fsn": ("sbuf", [128, C], "float16"),
    "fs": ("sbuf", [128, C], "bfloat16"),
    "o0": ("sbuf", [128, 20], "uint16"), "o1": ("sbuf", [128, 20], "uint16"), "o3": ("sbuf", [128, 20], "uint16"),
    "er": ("sbuf", [128, C], "float32"), "eh": ("sbuf", [128, C], "float32"), "sw": ("sbuf", [128, C], "bfloat16"),
    "scn": ("sbuf", [128, C], "float16"), "swn": ("sbuf", [128, C], "float16"), "fmn": ("sbuf", [128, C], "float16"), "fmr": ("sbuf", [128, C], "bfloat16"),
    "fo": ("sbuf", [128, 4 * C], "bfloat16"), "fh": ("sbuf", [128, 4 * C], "bfloat16"), "gp": ("sbuf", [128, 4 * C], "bfloat16"),
    "z": ("sbuf", [128, 4 * C], "bfloat16"), "zq": ("sbuf", [128, C], "float8_e4m3fn_x4"), "zp": ("sbuf", [128, C], "uint8"),
    "h": ("sbuf", [128, 4 * C], "bfloat16"),
    "pu": ("psum", [128, 2048], "float32"), "pw": ("psum", [128, 2048], "float32"),
}
LISTS = ["cw", "cwu", "col", "f0", "f1", "h0", "h1", "pif", "bd", "be", "bf", "swc", "fmv", "fw", "fd", "fe", "fn", "fv"]
SCRATCH["sml"] = ("sbuf", [128, 20 * len(LISTS)], "float32")
TABLES, PASSED = {}, {}
for _i, _l in enumerate(GROUPS):
    SCRATCH["p%d" % _i] = ("sbuf", [128, C * 2 ** len(_l)], "bfloat16")
    for _j, _k in enumerate(_l):
        TABLES[_k] = "m%d" % _k if _k >= 0 else "ml"
        PASSED[_k] = _l[:_j] if _j else GROUPS[_i - 1] if _i else []
        SCRATCH[TABLES[_k]] = ("sbuf", [128, C * 2 ** len(PASSED[_k])], "float32")
LAST = "p%d" % (len(GROUPS) - 1)
for _k in range(7):
    SCRATCH["l%d" % _k] = ("sbuf", [128, 20], "uint16")
for _r in range(ROUNDS + 1):
    if _r:
        SCRATCH["x%d" % _r] = ("sbuf", [128, 4 * C], "bfloat16")
    SCRATCH["xq%d" % _r] = ("sbuf", [128, C], "float8_e4m3fn_x4")
    SCRATCH["xp%d" % _r] = ("sbuf", [128, C], "uint8")
for _r in range(ROUNDS):
    SCRATCH["aq%d" % _r] = ("sbuf", [128, C], "float8_e4m3fn_x4")
    SCRATCH["ap%d" % _r] = ("sbuf", [128, C], "uint8")
    for _n in ("lp", "lb", "rp", "rb"):
        SCRATCH["%s%d" % (_n, _r)] = ("sbuf", [128, 20], "uint16")
SEMAPHORES = ["ev", "es", "et", "eg", "snd", "st"]
SEMAPHORES += ["%s%d" % (_n, _r) for _n in ("ax", "arp", "arb") for _r in range(ROUNDS)]
SEMAPHORES += ["ld_" + _n for _n in ("x", "u", "v", "nx", "mt", "wc", "ws")]

GATHER, SCAN2, SCAN4, ROW, SMALL = 0.58, 0.17, 0.33, 0.34, 0.08
HOP, SAME = 0.2, 0.1
SHARED = {}


def new_plan():
    return {"tasks": [], "w": {}, "r": {}}


def overlap(a, b):
    return a[0] < b[1] and b[0] < a[1]


def task(P, eng, dur, fn, reads, writes, kind="op", sem=None, inc=1, after=(), behind=()):
    def reg(x):
        return (x, 0, 1 << 20) if isinstance(x, str) else x
    n = len(P["tasks"])
    deps = {}
    for a in after:
        deps[a] = True
    rd, wr = [reg(x) for x in reads], [reg(x) for x in writes]
    for b, lo, hi in rd:
        for (l, h, t) in P["w"].get(b, []):
            if overlap((lo, hi), (l, h)):
                deps[t] = True
        if b in ("pu", "pw"):
            for (l, h, t) in P["r"].get(b, []):
                if overlap((lo, hi), (l, h)) and P["tasks"][t]["eng"] != eng:
                    deps.setdefault(t, False)
    for b, lo, hi in wr:
        for (l, h, t) in P["w"].get(b, []):
            if overlap((lo, hi), (l, h)):
                deps[t] = True
        for (l, h, t) in P["r"].get(b, []):
            if overlap((lo, hi), (l, h)):
                deps.setdefault(t, False)
    for b, lo, hi in wr:
        P["w"][b] = [e for e in P["w"].get(b, []) if not (lo <= e[0] and e[1] <= hi)] + [(lo, hi, n)]
        P["r"][b] = [e for e in P["r"].get(b, []) if not (lo <= e[0] and e[1] <= hi)]
    for b, lo, hi in rd:
        P["r"].setdefault(b, []).append((lo, hi, n))
    deps.pop(n, None)
    for a in behind:
        deps.setdefault(a, False)
    P["tasks"].append({"eng": eng, "dur": dur, "fn": fn, "deps": deps, "kind": kind, "sem": sem, "inc": inc})
    return n


def schedule(P, tries=5000):
    ts = P["tasks"]
    n = len(ts)
    lags = [[(d, HOP if ts[d]["eng"] != t["eng"] else SAME if t["deps"][d] else 0.0) for d in t["deps"]] for t in ts]
    succ = [[] for _ in range(n)]
    for i in range(n):
        for d, _ in lags[i]:
            succ[d].append(i)
    up = [t["dur"] for t in ts]
    for i in range(n - 1, -1, -1):
        for d, lag in lags[i]:
            up[d] = max(up[d], ts[d]["dur"] + lag + up[i])

    def place(rank):
        left = [len(x) for x in lags]
        ready = [i for i in range(n) if left[i] == 0]
        slots = {}
        start, end = [0.0] * n, [0.0] * n
        while ready:
            i = max(ready, key=lambda k: rank[k])
            ready.remove(i)
            t = ts[i]
            at, dur = 0.0, t["dur"]
            for d, lag in lags[i]:
                at = max(at, end[d] + lag)
            if t["eng"] != "net":
                line = slots.setdefault(t["eng"], [])
                k = len(line)
                while k and line[k - 1][1] > at:
                    k -= 1
                while True:
                    s = max(at, line[k - 1][1] if k else 0.0)
                    if k == len(line) or s + dur <= line[k][0] + 1e-9:
                        break
                    k += 1
                line.insert(k, (s, s + dur, i))
                at = s
            start[i], end[i] = at, at + dur
            for s in succ[i]:
                left[s] -= 1
                if left[s] == 0:
                    ready.append(s)
        return max(end), {e: [x[2] for x in line] for e, line in slots.items()}, start
    best, rank = place(up), up
    rng = np.random.default_rng(7)
    for _ in range(tries):
        at, width = rng.random() * max(up), [2, 5, 10][rng.integers(3)]
        part, step = [0.05, 0.15, 0.4][rng.integers(3)], [0.5, 1.5, 4.0][rng.integers(3)]
        hit, by = rng.random(n) < part, rng.standard_normal(n) * step
        trial = [float(rank[i] + by[i]) if hit[i] and abs(up[i] - at) < width else rank[i] for i in range(n)]
        got = place(trial)
        if got[0] <= best[0]:
            best, rank = got, trial
    return best[1], best[2], best[0]


def issue(P, order, start, g, T):
    ts = P["tasks"]
    queue = {"v": g.vector, "s": g.scalar, "t": g.tensor, "g": g, "y": g.sync}
    counter = {"v": "ev", "s": "es", "t": "et", "g": "eg"}
    mark, count = {}, {}
    for e, line in order.items():
        for i in line:
            t = ts[i]
            if t["kind"] == "op":
                count[counter[e]] = count.get(counter[e], 0) + 1
                mark[i] = (counter[e], count[counter[e]])
            else:
                mark[i] = (t["sem"], t["inc"])
    for i, t in enumerate(ts):
        if t["kind"] == "land":
            mark[i] = (t["sem"], t["inc"])
    seen = {e: {} for e in queue}
    known = {}
    pos = {i: k for line in order.values() for k, i in enumerate(line)}
    for i in sorted(pos, key=lambda i: (start[i], pos[i])):
        t = ts[i]
        e = t["eng"]
        q, have = queue[e], seen[e]
        need = {}
        for d, result in t["deps"].items():
            if ts[d]["kind"] == "send" or (ts[d]["eng"] == e and not result and ts[d]["kind"] == "op"):
                continue
            s, v = mark[d]
            need[s] = max(need.get(s, 0), v)
        for s, v in sorted(need.items()):
            if have.get(s, 0) < v:
                q.wait_ge(T.sem[s], v)
                have[s] = v
        for d, result in t["deps"].items():
            if d in known and not (ts[d]["eng"] == e and not result):
                for s, v in known[d].items():
                    have[s] = max(have.get(s, 0), v)
        k = dict(have)
        if t["kind"] == "op":
            t["fn"](q).then_inc(T.sem[mark[i][0]], 1)
            k[mark[i][0]] = max(k.get(mark[i][0], 0), mark[i][1])
        elif t["kind"] == "dma":
            t["fn"](q).then_inc(T.sem[t["sem"]], 16)
        else:
            t["fn"](q)
        if t["kind"] == "op":
            known[i] = k
    return count


def build(P, g, core, T, topo):
    rank = T.rank_of(core)
    n = len(T.cores)
    lists = {name: T.sml[:, 20 * i:20 * i + 20] for i, name in enumerate(LISTS)}
    col = T.sml[:, 20 * LISTS.index("col"):20 * LISTS.index("col") + 1]

    def L(name):
        return lists[name]

    def V(dur, fn, reads, writes, behind=()):
        return task(P, "v", dur, fn, reads, writes, behind=behind)

    def S(dur, fn, reads, writes):
        return task(P, "s", dur, fn, reads, writes)

    def E(dur, fn, reads, writes):
        return task(P, "t", dur, fn, reads, writes)

    def K(dur, fn, reads, writes):
        return task(P, "g", dur, fn, reads, writes)

    def every16(b):
        return T[b][:, 15:C:16]

    def at(b, a):
        return T[b][:, C * a:C * a + C]

    def copy(q, out, in_, **kw):
        return q.activation(out, in_, AF.Copy, **kw)

    def load(q, name, fn, writes):
        k = task(P, q, 0.07, fn, [], [], "dma", "ld_" + name, 16)
        task(P, "net", 2.0, None, [], writes, "land", "ld_" + name, 16, after=[k])

    load("y", "x", lambda q: q.dma_start(T.x0[:], T.x[:]), ["x0"])
    load("s", "nx", lambda q: q.dma_start(T.nxi[:], T.nx[:]), ["nxi"])
    load("y", "u", lambda q: q.dma_start(T.ut[:], T.u[:]), ["ut"])
    load("s", "mt", lambda q: q.dma_start(T.mti[:], T.mt[:]), ["mti"])
    load("y", "wc", lambda q: q.dma_start(T.wq[:].bitcast(dt.uint8), T.wc[:]), ["wq"])
    load("y", "ws", lambda q: q.dma_start(T.wp[:], T.ws[:]), ["wp"])
    load("y", "v", lambda q: q.dma_start(T.vt[:], T.v[:]), ["vt"])

    K(0.67, lambda q: q.iota(T.ji[:], [[1, C]], 0, -1), [], ["ji"])
    K(0.67, lambda q: q.iota(T.idr[:], [[1, C]], -160, 0, allow_small_or_imprecise_dtypes=True), [], ["idr"])
    K(0.17, lambda q: q.iota(T.pi[:], [[0, 20]], 0, 1), [], ["pi"])
    K(0.17, lambda q: q.iota(T.ci[:], [[16, 20]], 0, 0), [], ["ci"])
    K(0.15, lambda q: q.iota(T.ui[:], [[16, 8]], 0, 0), [], ["ui"])
    K(0.67, lambda q: q.iota(T.rs0[:], [[0, 20], [1, 16]], 0, 0, allow_small_or_imprecise_dtypes=True), [], ["rs0"])
    V(0.3, lambda q: q.memset(T.one[:], 1.0), [], ["one"])
    K(1.1, lambda q: q.affine_select(T.big[:], T.one[:], [[-1, 528]], A.is_equal, 0.0, 3, 4), ["one"], ["big"])
    V(ROW, lambda q: q.tensor_scalar(T.dg[:], T.ji[:], 15, None, A.bitwise_and), ["ji"], ["dg"])
    V(ROW, lambda q: q.tensor_scalar(T.t1[:], T.dg[:], 1.0, 320.0, A.is_equal, A.mult), ["dg"], ["t1"])
    V(ROW, lambda q: q.tensor_scalar(T.t2[:], T.dg[:], 0.0, -16384.0, A.is_equal, A.mult), ["dg"], ["t2"])
    V(2 * ROW, lambda q: q.tensor_tensor(T.wt[:], T.t1[:], T.t2[:], A.add), ["t1", "t2"], ["wt"])
    V(ROW, lambda q: q.tensor_scalar(T.mask[:], T.dg[:], 0.0, None, A.is_equal), ["dg"], ["mask"])
    V(ROW, lambda q: q.tensor_scalar(T.cap[:], T.mask[:], 2 * BIG, -BIG, A.mult, A.add), ["mask"], ["cap"])
    V(ROW, lambda q: q.tensor_scalar(T.rs[:], T.rs0[:], 1.0, None, A.min), ["rs0"], ["rs"])
    V(SMALL, lambda q: q.tensor_scalar(T.pa15[:], T.pi[:], 15, None, A.bitwise_and), ["pi"], ["pa15"])
    V(SMALL, lambda q: q.tensor_scalar(L("f0"), T.pa15[:], 15.0, 320.0, A.is_equal, A.mult), ["pa15"], ["f0"])
    V(SMALL, lambda q: q.tensor_scalar(L("col"), L("f0"), -160.0, None, A.add), ["f0"], ["col"])
    V(SMALL, lambda q: q.tensor_tensor(L("cw"), T.pa15[:], T.ci[:], A.add), ["pa15", "ci"], ["cw"])
    V(SMALL, lambda q: q.tensor_scalar(L("cwu"), L("cw"), 1.0 / C, None, A.mult), ["cw"], ["cwu"])
    V(SMALL, lambda q: q.tensor_copy(T.uo[:], T.ui[:]), ["ui"], ["uo"])
    for i in range(len(GROUPS)):
        S(ROW, lambda q, i=i: copy(q, at("p%d" % i, 0), T.idr[:]), ["idr"], [("p%d" % i, 0, 1)])
    for b in range(4):
        V(0.16, lambda q, b=b: q.quantize_mx(T.eq[:, 128 * b:128 * b + 128], T.ep[:, 128 * b:128 * b + 128], T.big[:, 3 - b:515 - b]),
          ["big"], [("eq", b, b + 1), ("ep", b, b + 1)])

    V(0.16, lambda q: q.quantize_mx(T.uq[:], T.up[:], T.ut[:]), ["ut"], ["uq", "up"])
    V(0.3, lambda q: q.tensor_copy(T.uqr[:].bitcast(dt.uint32), T.uq[:].bitcast(dt.uint32).indirect(T.uo[:])), ["uq", "uo"], ["uqr"])
    V(0.3, lambda q: q.tensor_copy(T.upr[:], T.up[:].indirect(T.uo[:])), ["up", "uo"], ["upr"])
    V(0.16, lambda q: q.quantize_mx(T.vq[:], T.vp[:], T.vt[:]), ["vt"], ["vq", "vp"])

    V(SMALL, lambda q: q.tensor_copy(T.l0[:], T.nxi[:]), ["nxi"], ["l0"])
    V(SMALL, lambda q: q.tensor_copy(L("fw"), T.nxi[:]), ["nxi"], ["fw"])
    V(SMALL, lambda q: q.tensor_copy(T.mt16[:], T.mti[:]), ["mti"], ["mt16"])
    V(SMALL, lambda q: q.tensor_copy(L("bd"), T.mti[:]), ["mti"], ["bd"])
    V(SMALL, lambda q: q.tensor_tensor(L("be"), L("bd"), L("cw"), A.min), ["bd", "cw"], ["be"])
    V(SMALL, lambda q: q.tensor_tensor(L("bf"), L("bd"), L("cw"), A.max), ["bd", "cw"], ["bf"])
    V(SMALL, lambda q: q.tensor_copy(T.lo16[:], L("be")), ["be"], ["lo16"])
    V(SMALL, lambda q: q.tensor_copy(T.hi16[:], L("bf")), ["bf"], ["hi16"])

    def row(out, a, win, i, k):
        S(GATHER, lambda q: copy(q, at(out, a), at(win, i).indirect(T["l%d" % k][:])), [(win, i, i + 1), "l%d" % k], [(out, a, a + 1)])

    def look(dst, win, i, k, off):
        S(GATHER, lambda q: copy(q, T[dst][:], T[win][:, C * i:C * k].indirect(T[off][:])), [(win, i, k), off], [dst])

    def running(dst, src):
        V(SCAN2, lambda q: q.tensor_tensor_scan(T[dst][:], T.rs[:], T[src][:], 0.0, A.mult, A.add), ["rs", src], [dst])

    def weighted(dst, src, a=0):
        V(SCAN2, lambda q: q.tensor_tensor_scan(T[dst][:], T.wt[:], at(src, a), 0.0, A.add, A.max), ["wt", (src, a, a + 1)], [dst])

    def at_f(k):
        return [("p%d" % i, 2 ** levels.index(k)) for i, levels in enumerate(GROUPS) if k in levels][0]

    def powers():
        row(*at_f(0), "idr", 0, 0)
        for k in range(6):
            l = "l%d" % (k + 1)
            row(*at_f(k + 1), *at_f(k), k)
            weighted("scn", *at_f(k + 1))
            V(SMALL, lambda q, l=l: q.tensor_scalar(T[l][:], every16("scn"), col, None, A.add), ["scn", "col"], [l])
        b, a = at_f(1)
        S(ROW, lambda q: copy(q, at(LAST, 2), at(b, a)), [(b, a, a + 1)], [(LAST, 2, 3)])
        for i, levels in enumerate(GROUPS):
            for j, k in enumerate(levels):
                for a2 in range(1, 2 ** j if k >= 0 else 0):
                    row("p%d" % i, 2 ** j + a2, "p%d" % i, a2, k)

    sent = [0]

    def send(r, pairs, sem, land, latency):
        dst, src = T.cores[(rank + r + 1) % n], T.cores[(rank - r - 1) % n]
        rid, pid, _ = topo.addr(dst)
        m = topo.mask(core, dst)
        ids = []
        for out, in_, name in pairs:
            ids.append(task(P, "g", 0.1, lambda q, out=out, in_=in_: q.remote_dma(out, in_, T.sem[sem], T.sem.snd, pid, rid, m), [name], [], "send"))
            sent[0] += len(topo.engines(core, dst))
        return task(P, "net", latency, None, [], land, "land", sem, len(topo.engines(src, core)) * len(pairs), after=ids)

    def compare(level, off, behind=()):
        win = TABLES[level]
        V(GATHER, lambda q: q.tensor_tensor(T.cb[:], T[win][:].indirect(T[off][:]), T.sm[:], A.is_le), [win, off, "sm"], ["cb"], behind)

    def mm(out, b, wq, wp, a, xq, xp, unit):
        E(0.35, lambda q: q.matmul_mx(T[out][:, BANK * b:BANK * b + C], T[wq][:, a:a + 128], T[wp][:, a:a + 128], T[xq][:], T[xp][:], True, True),
          [(wq, unit, unit + 1), (wp, unit, unit + 1), xq, xp], [(out, b, b + 1)])

    def bank(out, b):
        return T[out][:, BANK * b:BANK * b + C]

    powers()
    for r in range(ROUNDS):
        X, xq, xp, aq, ap = "x%d" % r, "xq%d" % r, "xp%d" % r, "aq%d" % r, "ap%d" % r
        lp, lb, rp, rb = "lp%d" % r, "lb%d" % r, "rp%d" % r, "rb%d" % r
        V(0.37, lambda q, xq=xq, xp=xp, X=X: q.quantize_mx(T[xq][:], T[xp][:], T[X][:]), [X], [xq, xp])
        send(r, [(T[aq][:].bitcast(dt.uint8), T[xq][:].bitcast(dt.uint8), xq), (T[ap][:], T[xp][:], xp)], "ax%d" % r, [aq, ap], 6.0)
        mm("pw", 0, "uqr", "upr", 0, xq, xp, 0)
        mm("pw", 1, "uqr", "upr", 0, xq, xp, 0)
        S(ROW, lambda q: copy(q, T.srow[:], bank("pw", 0)), [("pw", 0, 1)], ["srow"])
        V(ROW, lambda q: q.tensor_tensor(T.sm[:], bank("pw", 1), T.cap[:], A.min), [("pw", 1, 2), "cap"], ["sm"])
        V(GATHER, lambda q: q.tensor_copy(at("m0", 0), T.srow[:].indirect(T.l0[:])), ["srow", "l0"], [("m0", 0, 1)])
        S(GATHER, lambda q: copy(q, at("ml", 0), T.srow[:].indirect(T.l0[:])), ["srow", "l0"], [("ml", 0, 1)])
        for k in range(5):
            twin, m0, m1 = ("d%d" % (k % 2) if k else "ml"), "m%d" % k, "m%d" % (k + 1)
            V(GATHER, lambda q, k=k, twin=twin, m0=m0, m1=m1: q.tensor_tensor(at(m1, 0), at(m0, 0).indirect(T["l%d" % k][:]), at(twin, 0), A.max),
              [(m0, 0, 1), (twin, 0, 1), "l%d" % k], [(m1, 0, 1)])
            if k < 4:
                d = "d%d" % ((k + 1) % 2)
                S(ROW, lambda q, d=d, m1=m1: copy(q, at(d, 0), at(m1, 0)), [(m1, 0, 1)], [(d, 0, 1)])
        for k, passed in PASSED.items():
            for j, l in enumerate(passed):
                for a in range(2 ** j):
                    row(TABLES[k], 2 ** j + a, TABLES[k], a, l)
        for b in range(4):
            mm("pu", b, "eq", "ep", 128 * b, xq, xp, b)
            (V if b < 2 else S)(ROW, lambda q, b=b: (q.tensor_copy if b < 2 else lambda o, i: copy(q, o, i))(at("fo", b), bank("pu", b)),
                                [("pu", b, b + 1)], [("fo", b, b + 1)])
        for b in range(4):
            mm("pu", b, "eq", "ep", 128 * b, aq, ap, b)
            S(ROW, lambda q, b=b: copy(q, at("fh", b), bank("pu", b), scale=0.5), [("pu", b, b + 1)], [("fh", b, b + 1)])
        for i, levels in enumerate(GROUPS):
            place, last = "cwu" if i == 0 else "pif", i == len(GROUPS) - 1
            for j, k in enumerate(levels):
                if i == 0 and j == 0:
                    V(2 * ROW, lambda q: q.tensor_tensor(T.fb[:], at("m5", 0), T.sm[:], A.is_le), [("m5", 0, 1), "sm"], ["fb"])
                    running("fs", "fb")
                    V(GATHER, lambda q: q.tensor_tensor(T.cb[:], at("m5", 0).indirect(T.l5[:]), T.sm[:], A.is_le), [("m5", 0, 1), "l5", "sm"], ["cb"])
                    running("cs", "cb")
                    V(SMALL, lambda q: q.tensor_tensor(L("fv"), every16("cs"), every16("fs"), A.mult), ["cs", "fs"], ["fv"])
                else:
                    compare(k, off, behind)
                    running("cs", "cb")
                behind = []
                if k < 0:
                    break
                f, off = "f%d" % (j % 2), "o%d" % (j % 2)
                V(SMALL, lambda q, f=f, place=place, top=i + j == 0: q.tensor_tensor(L(f), L(place), L("fv") if top else every16("cs"), A.add),
                  [place, "cs", "fv"] if i + j == 0 else [place, "cs"], [f])
                V(SMALL, lambda q, f=f, off=off, j=j: q.tensor_scalar(T[off][:], L(f), float(C * 2 ** j), 0.25, A.mult, A.add), [f], [off])
                if j + 1 < len(levels) and levels[j + 1] >= 0:
                    place = "h%d" % (j % 2)
                    behind = [V(SMALL, lambda q, f=f, place=place: q.tensor_scalar(L(place), L(f), 0.5, None, A.mult), [f], [place])]
                if j + 1 < len(levels) and levels[j + 1] < 0:
                    look("pr", LAST, 0, 2, off)
                    look("fr", LAST, 1, 3, off)
                    weighted("pws", "pr")
                    V(SMALL, lambda q, lp=lp: q.tensor_scalar(T[lp][:], every16("pws"), col, None, A.add), ["pws", "col"], [lp])
                    send(r, [(T[rp][:], T[lp][:], lp)], "arp%d" % r, [rp], 2.6)
                    weighted("fsn", "fr")
                    V(SMALL, lambda q: q.tensor_scalar(L("fv"), every16("fsn"), col, None, A.add), ["fsn", "col"], ["fv"])
                    V(SMALL, lambda q: q.tensor_tensor(L("bd"), L("cw"), L("fv"), A.subtract), ["cw", "fv"], ["bd"])
            if not last:
                look("pb", "p%d" % i, 0, 2 ** len(levels), off)
                weighted("psn", "pb")
                V(SMALL, lambda q: q.tensor_scalar(L("pif"), every16("psn"), col, 1.0 / C, A.add, A.mult), ["psn", "col"], ["pif"])
        V(SMALL, lambda q: q.tensor_tensor(L("be"), L("bd"), every16("cs"), A.mult), ["bd", "cs"], ["be"])
        V(SMALL, lambda q: q.tensor_tensor(L("bf"), L("be"), L("fv"), A.add), ["be", "fv"], ["bf"])
        V(SMALL, lambda q, lb=lb: q.tensor_copy(T[lb][:], L("bf")), ["bf"], [lb])
        send(r, [(T[rb][:], T[lb][:], lb)], "arb%d" % r, [rb], 2.6)
        S(GATHER, lambda q, lb=lb: copy(q, T.er[:], T.srow[:].indirect(T[lb][:])), ["srow", lb], ["er"])
        S(GATHER, lambda q: copy(q, T.eh[:], T.er[:].indirect(T.hi16[:])), ["er", "hi16"], ["eh"])
        V(GATHER, lambda q: q.tensor_tensor(T.sw[:], T.er[:].indirect(T.lo16[:]), T.eh[:], A.is_gt), ["er", "eh", "lo16"], ["sw"])
        weighted("swn", "sw")
        V(SMALL, lambda q: q.tensor_scalar(L("swc"), every16("swn"), col, -160.0, A.add, A.add), ["swn", "col"], ["swc"])
        S(GATHER, lambda q: copy(q, T.fmr[:], at(*at_f(0)).indirect(T.mt16[:])), [at_f(0) + (at_f(0)[1] + 1,), "mt16"], ["fmr"])
        weighted("fmn", "fmr")
        V(SMALL, lambda q: q.tensor_scalar(L("fmv"), every16("fmn"), col, None, A.add), ["fmn", "col"], ["fmv"])
        fw, fn = ("fw", "fn") if r % 2 == 0 else ("fn", "fw")
        V(SMALL, lambda q, fw=fw: q.tensor_tensor(L("fd"), L("fmv"), L(fw), A.subtract), ["fmv", fw], ["fd"])
        V(SMALL, lambda q: q.tensor_tensor(L("fe"), L("fd"), L("swc"), A.mult), ["fd", "swc"], ["fe"])
        V(SMALL, lambda q, fw=fw, fn=fn: q.tensor_tensor(L(fn), L(fw), L("fe"), A.add), [fw, "fe"], [fn])
        V(SMALL, lambda q, fn=fn: q.tensor_copy(T.l0[:], L(fn)), [fn], ["l0"])
        if r < ROUNDS - 1:
            powers()
        else:
            S(GATHER, lambda q: copy(q, T.er[:], T.idr[:].indirect(T.l0[:]), bias=160.0), ["idr", "l0"], ["er"])
            task(P, "y", 0.07, lambda q: q.dma_start(T.nf[:], T.er[0:128:16, :]), ["er"], [], "dma", "st", 16)
        for b in range(4):
            S(GATHER, lambda q, b=b, rp=rp: copy(q, at("gp", b), at("fh", b).indirect(T[rp][:])), [("fh", b, b + 1), rp], [("gp", b, b + 1)])
            V(GATHER, lambda q, b=b, rb=rb: q.tensor_tensor(T.z[:, b:4 * C:4], at("fh", b).indirect(T[rb][:]), at("gp", b), A.add),
              [("fh", b, b + 1), rb, ("gp", b, b + 1)], [("z", b, b + 1)])
        V(0.37, lambda q: q.quantize_mx(T.zq[:], T.zp[:], T.z[:]), ["z"], ["zq", "zp"])
        Y = "x%d" % (r + 1)
        for b in range(4):
            mm("pw", b, "wq", "wp", 128 * b, "zq", "zp", b)
            S(ROW, lambda q, b=b: copy(q, at("h", b), bank("pw", b), scale=0.03125), [("pw", b, b + 1)], [("h", b, b + 1)])
            V(GATHER, lambda q, b=b, lb=lb, Y=Y: q.tensor_tensor(T[Y][:, b:4 * C:4], at("h", b).indirect(T[lb][:]), at("fo", b), A.add),
              [("h", b, b + 1), lb, ("fo", b, b + 1)], [(Y, b, b + 1)])
    xq, xp, X = "xq%d" % ROUNDS, "xp%d" % ROUNDS, "x%d" % ROUNDS
    V(0.37, lambda q, xq=xq, xp=xp, X=X: q.quantize_mx(T[xq][:], T[xp][:], T[X][:]), [X], [xq, xp])
    task(P, "y", 0.07, lambda q: q.dma_start(T.oc[:], T[xq][:].bitcast(dt.uint8)), [xq], [], "dma", "st", 16)
    for k in range(4):
        task(P, "y" if k % 2 else "s", 0.07, lambda q, k=k: q.dma_start(T.osc[4 * k:4 * k + 4, :], T[xp][32 * k:32 * k + 4, :]), [xp], [], "dma", "st", 16)
    mm("pw", 0, "vq", "vp", 0, xq, xp, 0)
    V(ROW, lambda q: q.tensor_copy(T.eh[:], bank("pw", 0)), [("pw", 0, 1)], ["eh"])
    task(P, "y", 0.07, lambda q: q.dma_start(T.y[:], T.eh[:]), ["eh"], [], "dma", "st", 16)
    return sent[0]


def rank_program(g, core, T, topo):
    if T.rank_of(core) is None:
        return
    P = new_plan()
    sent = build(P, g, core, T, topo)
    if "order" not in SHARED:
        SHARED["order"] = schedule(P)
    order, start, _ = SHARED["order"]
    count = issue(P, order, start, g, T)
    g.sync.wait_ge(T.sem.st, 16 * sum(1 for t in P["tasks"] if t["sem"] == "st"))
    for s, k in sorted(count.items()):
        g.sync.wait_ge(T.sem[s], k)
    g.wait_ge(T.sem.snd, sent)
